import numpy as np
import ml_dtypes


def mxq(x, axis, fmt="e4m3"):
    dtype, down = {"e4m3": (ml_dtypes.float8_e4m3fn, 7), "e5m2": (ml_dtypes.float8_e5m2, 14)}[fmt]
    v = np.moveaxis(np.asarray(x, np.float32).astype(ml_dtypes.bfloat16).astype(np.float64), axis, -1)
    blocks = v.reshape(v.shape[:-1] + (-1, 32))
    amax = np.abs(blocks).max(-1, keepdims=True)
    byte = np.maximum(np.where(amax > 0, np.frexp(amax)[1] - 1 + 127, 0) - down, 1)
    scale = np.exp2(byte - 127.0)
    codes = (blocks / scale).astype(np.float32).astype(dtype).astype(np.float64)
    return np.moveaxis((codes * scale).reshape(v.shape), -1, axis)


WIDE = False


def mx_kscale(k):
    if not WIDE:
        return np.ones(k)
    levels = np.array([10, -10, 5, -5, 0])
    if k % 512:
        return np.exp2(np.random.permutation(np.resize(levels, k // 32))).repeat(32)
    a = np.empty((k // 512, 16))
    for p in range(k // 512):
        a[p, :8] = np.random.permutation(np.resize(levels, 8))
        for g in range(8):
            far = levels[np.abs(levels - a[p, g]) >= 10]
            a[p, g + 8] = far[np.random.randint(len(far))]
    return np.exp2(a.ravel()).repeat(32)


def f64(x):
    return np.asarray(x).astype(np.float64)


def striped(idx):
    return np.tile(idx.reshape(-1, 16).T, (8, 1)).astype(np.uint16)


def unstriped(offs):
    return offs[:16].T.reshape(-1).astype(np.int64)


def pack_weight(w):
    k, n = w.shape
    w = f64(np.asarray(w, np.float32).astype(ml_dtypes.bfloat16)).reshape(k // 32, 32, n)
    amax = np.abs(w).max(1)
    byte = np.clip(np.where(amax > 0, np.frexp(amax)[1] - 1 + 127 - 7, 1), 1, 254)
    scaled = (w * np.exp2(127.0 - byte)[:, None, :]).reshape(k, n).astype(np.float32)
    words = np.ascontiguousarray(scaled.reshape(k // 512, 128, 4, n).transpose(0, 1, 3, 2)).astype(ml_dtypes.float8_e4m3fn).view(np.uint8)
    return words, np.ascontiguousarray(byte.astype(np.uint8).reshape(k // 512, 16, n))


def unpack_weight(words, scales):
    g, p, n, _ = words.shape
    vals = np.ascontiguousarray(words).view(ml_dtypes.float8_e4m3fn).astype(np.float64) * np.repeat(np.exp2(scales.astype(np.float64) - 127.0), 8, axis=1)[..., None]
    return vals.transpose(0, 1, 3, 2).reshape(g * 512, n)


def silu(v):
    return v / (1.0 + np.exp(-np.maximum(v, -700.0)))


K, T, E, C, N = 1024, 2048, 16, 256, 128


def by_expert(wq, xq):
    return np.concatenate([wq[e].T @ xq[:, e * C:(e + 1) * C] for e in range(E)], axis=1)


def setup_inputs():
    n = np.random.standard_normal
    s = mx_kscale(K)[:, None]
    first = np.random.permutation(np.repeat(np.arange(E), T // E))
    second = (first + 1 + np.random.permutation(np.repeat(np.arange(E - 1), -(-T // (E - 1)))[:T])) % E
    while np.bincount(second, minlength=E).max() != T // E:
        load = np.bincount(second, minlength=E); hi, lo = int(load.argmax()), int(load.argmin())
        t = np.flatnonzero((second == hi) & (first != lo))[0]; second[t] = lo
    slot_token = np.empty(E * C, np.int64); pos = np.empty((2, T), np.int64); fill = np.zeros(E, np.int64)
    place = np.stack([np.random.permutation(C) for _ in range(E)])
    for r, deal in enumerate((first, second)):
        for t in np.random.permutation(T):
            e = deal[t]; j = e * C + place[e, fill[e]]; fill[e] += 1; slot_token[j] = t; pos[r, t] = j
    g = np.random.uniform(0.2, 0.8, T)
    packed = [pack_weight(m) for m in n((E, K, N)) / np.sqrt(K) / s[None]]
    return {
        "xT": (n((K, T)) * s).astype(np.float32),
        "w_words": np.stack([m[0] for m in packed]),
        "w_scales": np.stack([m[1] for m in packed]),
        "b": (0.3 * n((N, E))).astype(np.float32),
        "gate": np.stack([np.tile(g, (N, 1)), np.tile(1.0 - g, (N, 1))]).astype(np.float32),
        "offs": striped(slot_token),
        "pos1": striped(pos[0]),
        "pos2": striped(pos[1]),
    }


def reference(xT, w_words, w_scales, b, gate, offs, pos1, pos2):
    idx = unstriped(offs)
    xq = mxq(f64(xT)[:, idx], 0, "e4m3")
    w = np.stack([unpack_weight(w_words[e], w_scales[e]) for e in range(E)])
    y = by_expert(w, xq)
    y = silu(y + np.repeat(f64(b), C, axis=1))
    return f64(gate[0]) * y[:, unstriped(pos1)] + f64(gate[1]) * y[:, unstriped(pos2)]

@@ -1,0 +1,169 @@
+from contextlib import ExitStack
+
+import concourse.mybir as mybir
+from concourse.masks import make_identity
+
+K, T, E, C, N = 1024, 2048, 16, 256, 128
+P = 128
+PASSES = 2
+SLOTS = E * C
+FLOPS = 2 * SLOTS * K * N
+
+F32 = mybir.dt.float32
+BF16 = mybir.dt.bfloat16
+I32 = mybir.dt.int32
+U32 = mybir.dt.uint32
+U16 = mybir.dt.uint16
+U8 = mybir.dt.uint8
+FP8X4 = mybir.dt.float8_e4m3fn_x4
+MULT = mybir.AluOpType.mult
+SILU = mybir.ActivationFunctionType.Silu
+
+CHUNKS = (
+    ((1024, 640), (512, 320), (256, 160), (256, 160)),
+    ((512, 0), (512, 0), (512, 0), (256, 0), (256, 160)),
+)
+WORD0_CUTS = (1536, 1536, 1024)
+SCALE_CUTS = (1536, 1536, 1024)
+WORD1_CUTS = (1536, 1536, 768, 256)
+OUT_CUTS = ((512, True), (512, True), (512, True), (256, False), (256, False))
+
+
+def tile_routed_moe_kernel(tc, xT, w_words, w_scales, b, gate, offs, pos1, pos2, out):
+    nc = tc.nc
+    with ExitStack() as ctx:
+        lists = ctx.enter_context(tc.tile_pool(name="lists", bufs=1))
+        keep = ctx.enter_context(tc.tile_pool(name="keep", bufs=1))
+        raws = ctx.enter_context(tc.tile_pool(name="raws", bufs=1))
+        grouped = ctx.enter_context(tc.tile_pool(name="grouped", bufs=4))
+        psum = ctx.enter_context(tc.psum_pool(name="psum", bufs=4))
+
+        offs_sb = lists.tile([P, SLOTS // 16], U16, name="offs_sb")
+        pos1_sb = lists.tile([P, T // 16], U16, name="pos1_sb")
+        pos2_sb = lists.tile([P, T // 16], U16, name="pos2_sb")
+
+        words = [keep.tile([P, T], U32, name="words%d" % a, align_bytes=64) for a in range(PASSES)]
+        scales = keep.tile([P, T], U8, name="scales", align_bytes=64)
+        slot_words = [keep.tile([P, SLOTS], U32, name="slot_words%d" % a, align_bytes=64) for a in range(PASSES)]
+        slot_scales = keep.tile([P, SLOTS], U8, name="slot_scales", align_bytes=64)
+        w_sb = keep.tile([P, E, PASSES, N], I32, name="w_sb", align_bytes=64)
+        ws_sb = keep.tile([P, E, N], U8, name="ws_sb", align_bytes=64)
+        b_sb = keep.tile([P, E], F32, name="b_sb")
+        gate_sb = [keep.tile([P, T], F32, name="gate_sb%d" % r) for r in range(2)]
+        y = keep.tile([P, SLOTS], F32, name="y")
+
+        ident = keep.tile([P, P], F32, name="ident")
+        nc.gpsimd.memset(scales[:], 0)
+        nc.gpsimd.memset(ws_sb[:], 0)
+        make_identity(nc, ident[:])
+
+        def load(a):
+            got = []
+            t0 = 0
+            rows = xT[a * 512 : (a + 1) * 512, :].rearrange("(p j) t -> p j t", j=4)
+            for n, v in CHUNKS[a]:
+                raw = raws.tile([P, 4, n], F32, name="raw%d_%d" % (a, t0))
+                nc.sync.dma_start(out=raw[:], in_=rows[:, :, t0 : t0 + n])
+                got.append((raw, t0, n, v))
+                t0 += n
+            return got
+
+        def interleave(copy, g, raw, lo, hi):
+            copy(
+                out=g[:, lo:hi, :].rearrange("p (c i) j -> p c j i", i=4),
+                in_=raw[:, :, lo:hi].rearrange("p j (c i) -> p c j i", i=4),
+            )
+
+        def quantise(a, chunk):
+            raw, t0, n, v = chunk
+            g = grouped.tile([P, n, 4], BF16, name="g", align_bytes=64)
+            interleave(nc.scalar.copy, g, raw, v, n)
+            if v:
+                interleave(nc.vector.tensor_copy, g, raw, 0, v)
+            nc.vector.quantize_mx(
+                out=words[a][:, t0 : t0 + n].bitcast(FP8X4),
+                scales=scales[4 * a : P, t0 : t0 + n],
+                in_=g[:].rearrange("p t j -> p (t j)"),
+            )
+
+        def gather_words(a, s0, n):
+            cols = slice(s0, s0 + n)
+            nc.vector.tensor_copy(slot_words[a][:, cols], words[a][:].indirect(offs_sb[:, s0 // 16 : (s0 + n) // 16]))
+
+        def gather_scales(s0, n):
+            cols = slice(s0, s0 + n)
+            nc.vector.tensor_copy(slot_scales[:, cols], scales[:].indirect(offs_sb[:, s0 // 16 : (s0 + n) // 16]))
+
+        def expert(e):
+            cols = slice(e * C, (e + 1) * C)
+            acc = psum.tile([P, C], F32, name="acc")
+            for a in range(PASSES):
+                nc.tensor.matmul_mx(
+                    out=acc[:],
+                    lhsT=w_sb[:, e, a, :].bitcast(FP8X4),
+                    lhsT_scale=ws_sb[4 * a : P, e, :],
+                    rhs=slot_words[a][:, cols].bitcast(FP8X4),
+                    rhs_scale=slot_scales[4 * a : P, cols],
+                    start=(a == 0),
+                    stop=(a == PASSES - 1),
+                )
+            nc.scalar.activation(out=y[:, cols], in_=acc[:], func=SILU, bias=b_sb[:, e : e + 1])
+
+        chunks0 = load(0)
+        nc.sync.dma_start(offs_sb[:], offs)
+        chunks1 = load(1)
+        for a in range(PASSES):
+            for q in range(4):
+                nc.sync.dma_start(
+                    out=ws_sb[32 * q + 4 * a : 32 * q + 4 * a + 4, :, :].bitcast(I32),
+                    in_=w_scales[:, a, 4 * q : 4 * q + 4, :].rearrange("e q n -> q e n").bitcast(I32),
+                )
+        for h in range(2):
+            es = slice(h * E // 2, (h + 1) * E // 2)
+            nc.sync.dma_start(
+                out=w_sb[:, es, :, :].rearrange("p e a n -> p (e a) n"),
+                in_=w_words[es].rearrange("e a p n r -> p (e a) (n r)").bitcast(I32),
+            )
+        nc.sync.dma_start(b_sb[:], b)
+        nc.sync.dma_start(pos1_sb[:], pos1)
+        nc.sync.dma_start(pos2_sb[:], pos2)
+        for r in range(2):
+            nc.sync.dma_start(gate_sb[r][:], gate[r])
+
+        for chunk in chunks0:
+            quantise(0, chunk)
+        s0 = 0
+        for n in WORD0_CUTS:
+            gather_words(0, s0, n)
+            s0 += n
+        for chunk in chunks1:
+            quantise(1, chunk)
+        s0 = 0
+        for n in SCALE_CUTS:
+            gather_scales(s0, n)
+            s0 += n
+        s0 = 0
+        for n in WORD1_CUTS:
+            gather_words(1, s0, n)
+            for e in range(s0 // C, (s0 + n) // C):
+                expert(e)
+            s0 += n
+
+        t0 = 0
+        for i, (n, on_tensor) in enumerate(OUT_CUTS):
+            cols = slice(t0, t0 + n)
+            at = slice(t0 // 16, (t0 + n) // 16)
+            u = keep.tile([P, n], F32, name="u%d" % i)
+            v = keep.tile([P, n], F32, name="v%d" % i)
+            o = keep.tile([P, n], F32, name="o%d" % i)
+            nc.vector.tensor_tensor(u[:], y[:].indirect(pos1_sb[:, at]), gate_sb[0][:, cols], MULT)
+            nc.vector.tensor_tensor(v[:], y[:].indirect(pos2_sb[:, at]), gate_sb[1][:, cols], MULT)
+            if on_tensor:
+                both = psum.tile([P, n], F32, name="both")
+                nc.tensor.matmul(both[:], ident[:], u[:], start=True, stop=False)
+                nc.tensor.matmul(both[:], ident[:], v[:], start=False, stop=True)
+                nc.scalar.copy(out=o[:], in_=both[:])
+            else:
+                nc.vector.tensor_add(out=o[:], in0=u[:], in1=v[:])
+            nc.sync.dma_start(out=out[:, cols], in_=o[:])
+            t0 += n

@@ -20,13 +20,12 @@ MULT = mybir.AluOpType.mult
 SILU = mybir.ActivationFunctionType.Silu
 
 CHUNKS = (
-    ((1024, 640), (512, 320), (256, 160), (256, 160)),
-    ((512, 0), (512, 0), (512, 0), (256, 0), (256, 160)),
+    ((768, 256, (256, 512)), (640, 320, (128, 512)), (384, 224, (128, 256)), (256, 176, (256,))),
+    ((512, 0, (512,)), (512, 0, (512,)), (512, 0, (512,)), (512, 0, (256, 256))),
 )
 WORD0_CUTS = (1536, 1536, 1024)
-SCALE_CUTS = (1536, 1536, 1024)
-WORD1_CUTS = (1536, 1536, 768, 256)
-OUT_CUTS = ((512, True), (512, True), (512, True), (256, False), (256, False))
+LAST_GATHERS = ((1536, (1536,)), (1536, (1536,)), (1024, (512, 256, 256)))
+OUT_CUTS = ((512, "matmul"), (512, "matmul"), (512, "matmul"), (256, "vector"), (256, "vector"))
 
 
 def tile_routed_moe_kernel(tc, xT, w_words, w_scales, b, gate, offs, pos1, pos2, out):
@@ -34,14 +33,13 @@ def tile_routed_moe_kernel(tc, xT, w_words, w_scales, b, gate, offs, pos1, pos2,
     with ExitStack() as ctx:
         lists = ctx.enter_context(tc.tile_pool(name="lists", bufs=1))
         keep = ctx.enter_context(tc.tile_pool(name="keep", bufs=1))
-        raws = ctx.enter_context(tc.tile_pool(name="raws", bufs=1))
-        grouped = ctx.enter_context(tc.tile_pool(name="grouped", bufs=4))
         psum = ctx.enter_context(tc.psum_pool(name="psum", bufs=4))
 
         offs_sb = lists.tile([P, SLOTS // 16], U16, name="offs_sb")
         pos1_sb = lists.tile([P, T // 16], U16, name="pos1_sb")
         pos2_sb = lists.tile([P, T // 16], U16, name="pos2_sb")
 
+        grouped = [keep.tile([P, T, 4], BF16, name="grouped%d" % a, align_bytes=64) for a in range(PASSES)]
         words = [keep.tile([P, T], U32, name="words%d" % a, align_bytes=64) for a in range(PASSES)]
         scales = keep.tile([P, T], U8, name="scales", align_bytes=64)
         slot_words = [keep.tile([P, SLOTS], U32, name="slot_words%d" % a, align_bytes=64) for a in range(PASSES)]
@@ -53,38 +51,43 @@ def tile_routed_moe_kernel(tc, xT, w_words, w_scales, b, gate, offs, pos1, pos2,
         y = keep.tile([P, SLOTS], F32, name="y")
 
         ident = keep.tile([P, P], F32, name="ident")
-        nc.gpsimd.memset(scales[:], 0)
-        nc.gpsimd.memset(ws_sb[:], 0)
+        nc.vector.memset(scales[:].bitcast(I32), 0)
+        nc.vector.memset(ws_sb[:].rearrange("p e n -> p (e n)").bitcast(I32), 0)
         make_identity(nc, ident[:])
 
         def load(a):
             got = []
             t0 = 0
             rows = xT[a * 512 : (a + 1) * 512, :].rearrange("(p j) t -> p j t", j=4)
-            for n, v in CHUNKS[a]:
-                raw = raws.tile([P, 4, n], F32, name="raw%d_%d" % (a, t0))
+            for n, v, widths in CHUNKS[a]:
+                raw = keep.tile([P, 4, n], F32, name="raw%d_%d" % (a, t0))
                 nc.sync.dma_start(out=raw[:], in_=rows[:, :, t0 : t0 + n])
-                got.append((raw, t0, n, v))
+                got.append((raw, t0, n, v, widths))
                 t0 += n
             return got
 
-        def interleave(copy, g, raw, lo, hi):
+        def interleave(copy, a, raw, t0, lo, hi):
             copy(
-                out=g[:, lo:hi, :].rearrange("p (c i) j -> p c j i", i=4),
+                out=grouped[a][:, t0 + lo : t0 + hi, :].rearrange("p (c i) j -> p c j i", i=4),
                 in_=raw[:, :, lo:hi].rearrange("p j (c i) -> p c j i", i=4),
             )
 
         def quantise(a, chunk):
-            raw, t0, n, v = chunk
-            g = grouped.tile([P, n, 4], BF16, name="g", align_bytes=64)
-            interleave(nc.scalar.copy, g, raw, v, n)
+            raw, t0, n, v, widths = chunk
+            lo = 0
+            for m in widths:
+                if lo + m > v:
+                    interleave(nc.scalar.copy, a, raw, t0, max(lo, v), lo + m)
+                lo += m
             if v:
-                interleave(nc.vector.tensor_copy, g, raw, 0, v)
-            nc.vector.quantize_mx(
-                out=words[a][:, t0 : t0 + n].bitcast(FP8X4),
-                scales=scales[4 * a : P, t0 : t0 + n],
-                in_=g[:].rearrange("p t j -> p (t j)"),
-            )
+                interleave(nc.vector.tensor_copy, a, raw, t0, 0, v)
+            for m in widths:
+                nc.vector.quantize_mx(
+                    out=words[a][:, t0 : t0 + m].bitcast(FP8X4),
+                    scales=scales[4 * a : P, t0 : t0 + m],
+                    in_=grouped[a][:, t0 : t0 + m, :].rearrange("p t j -> p (t j)"),
+                )
+                t0 += m
 
         def gather_words(a, s0, n):
             cols = slice(s0, s0 + n)
@@ -139,18 +142,16 @@ def tile_routed_moe_kernel(tc, xT, w_words, w_scales, b, gate, offs, pos1, pos2,
         for chunk in chunks1:
             quantise(1, chunk)
         s0 = 0
-        for n in SCALE_CUTS:
-            gather_scales(s0, n)
-            s0 += n
-        s0 = 0
-        for n in WORD1_CUTS:
-            gather_words(1, s0, n)
-            for e in range(s0 // C, (s0 + n) // C):
-                expert(e)
-            s0 += n
+        for n_scales, word_cuts in LAST_GATHERS:
+            gather_scales(s0, n_scales)
+            for n in word_cuts:
+                gather_words(1, s0, n)
+                for e in range(s0 // C, (s0 + n) // C):
+                    expert(e)
+                s0 += n
 
         t0 = 0
-        for i, (n, on_tensor) in enumerate(OUT_CUTS):
+        for i, (n, adder) in enumerate(OUT_CUTS):
             cols = slice(t0, t0 + n)
             at = slice(t0 // 16, (t0 + n) // 16)
             u = keep.tile([P, n], F32, name="u%d" % i)
@@ -158,7 +159,7 @@ def tile_routed_moe_kernel(tc, xT, w_words, w_scales, b, gate, offs, pos1, pos2,
             o = keep.tile([P, n], F32, name="o%d" % i)
             nc.vector.tensor_tensor(u[:], y[:].indirect(pos1_sb[:, at]), gate_sb[0][:, cols], MULT)
             nc.vector.tensor_tensor(v[:], y[:].indirect(pos2_sb[:, at]), gate_sb[1][:, cols], MULT)
-            if on_tensor:
+            if adder == "matmul":
                 both = psum.tile([P, n], F32, name="both")
                 nc.tensor.matmul(both[:], ident[:], u[:], start=True, stop=False)
                 nc.tensor.matmul(both[:], ident[:], v[:], start=False, stop=True)

@@ -25,7 +25,8 @@ CHUNKS = (
 )
 WORD0_CUTS = (1536, 1536, 1024)
 LAST_GATHERS = ((1536, (1536,)), (1536, (1536,)), (1024, (512, 256, 256)))
-OUT_CUTS = ((512, "matmul"), (512, "matmul"), (512, "matmul"), (256, "vector"), (256, "vector"))
+TENSOR_ADDS = (256, 512, 512, 128)
+VECTOR_ADDS = (384, 256)
 
 
 def tile_routed_moe_kernel(tc, xT, w_words, w_scales, b, gate, offs, pos1, pos2, out):
@@ -97,9 +98,9 @@ def tile_routed_moe_kernel(tc, xT, w_words, w_scales, b, gate, offs, pos1, pos2,
             cols = slice(s0, s0 + n)
             nc.vector.tensor_copy(slot_scales[:, cols], scales[:].indirect(offs_sb[:, s0 // 16 : (s0 + n) // 16]))
 
-        def expert(e):
-            cols = slice(e * C, (e + 1) * C)
-            acc = psum.tile([P, C], F32, name="acc")
+        def expert(e, lo, hi):
+            cols = slice(e * C + lo, e * C + hi)
+            acc = psum.tile([P, hi - lo], F32, name="acc")
             for a in range(PASSES):
                 nc.tensor.matmul_mx(
                     out=acc[:],
@@ -147,24 +148,40 @@ def tile_routed_moe_kernel(tc, xT, w_words, w_scales, b, gate, offs, pos1, pos2,
             for n in word_cuts:
                 gather_words(1, s0, n)
                 for e in range(s0 // C, (s0 + n) // C):
-                    expert(e)
+                    step = C // 2 if e == E - 1 else C
+                    for lo in range(0, C, step):
+                        expert(e, lo, lo + step)
                 s0 += n
 
+        def shares(name, t0, n):
+            return keep.tile([P, n], F32, name="%s%d" % (name, t0))
+
+        def weigh(dst, r, pos_sb, t0, n):
+            nc.vector.tensor_tensor(
+                dst, y[:].indirect(pos_sb[:, t0 // 16 : (t0 + n) // 16]), gate_sb[r][:, t0 : t0 + n], MULT
+            )
+
         t0 = 0
-        for i, (n, adder) in enumerate(OUT_CUTS):
-            cols = slice(t0, t0 + n)
-            at = slice(t0 // 16, (t0 + n) // 16)
-            u = keep.tile([P, n], F32, name="u%d" % i)
-            v = keep.tile([P, n], F32, name="v%d" % i)
-            o = keep.tile([P, n], F32, name="o%d" % i)
-            nc.vector.tensor_tensor(u[:], y[:].indirect(pos1_sb[:, at]), gate_sb[0][:, cols], MULT)
-            nc.vector.tensor_tensor(v[:], y[:].indirect(pos2_sb[:, at]), gate_sb[1][:, cols], MULT)
-            if adder == "matmul":
-                both = psum.tile([P, n], F32, name="both")
-                nc.tensor.matmul(both[:], ident[:], u[:], start=True, stop=False)
-                nc.tensor.matmul(both[:], ident[:], v[:], start=False, stop=True)
-                nc.scalar.copy(out=o[:], in_=both[:])
-            else:
-                nc.vector.tensor_add(out=o[:], in0=u[:], in1=v[:])
-            nc.sync.dma_start(out=out[:, cols], in_=o[:])
+        for n in TENSOR_ADDS:
+            u, v, o = shares("u", t0, n), shares("v", t0, n), shares("o", t0, n)
+            weigh(u[:], 0, pos1_sb, t0, n)
+            weigh(v[:], 1, pos2_sb, t0, n)
+            both = psum.tile([P, n], F32, name="both")
+            nc.tensor.matmul(both[:], ident[:], u[:], start=True, stop=False)
+            nc.tensor.matmul(both[:], ident[:], v[:], start=False, stop=True)
+            nc.scalar.copy(out=o[:], in_=both[:])
+            nc.sync.dma_start(out=out[:, t0 : t0 + n], in_=o[:])
             t0 += n
+
+        rest = T - t0
+        u, v, o = shares("u", t0, rest), shares("v", t0, rest), shares("o", t0, rest)
+        weigh(u[:], 0, pos1_sb, t0, rest)
+        pieces = []
+        lo = 0
+        for n in VECTOR_ADDS:
+            pieces.append(slice(lo, lo + n))
+            weigh(v[:, lo : lo + n], 1, pos2_sb, t0 + lo, n)
+            lo += n
+        for cols in pieces:
+            nc.vector.tensor_add(out=o[:, cols], in0=u[:, cols], in1=v[:, cols])
+            nc.sync.dma_start(out=out[:, t0 + cols.start : t0 + cols.stop], in_=o[:, cols])

@@ -25,8 +25,8 @@ CHUNKS = (
 )
 WORD0_CUTS = (1536, 1536, 1024)
 LAST_GATHERS = ((1536, (1536,)), (1536, (1536,)), (1024, (512, 256, 256)))
-TENSOR_ADDS = (256, 512, 512, 128)
-VECTOR_ADDS = (384, 256)
+TENSOR_ADDS = (256, 512, 512, 256)
+VECTOR_ADDS = (256, 256)
 
 
 def tile_routed_moe_kernel(tc, xT, w_words, w_scales, b, gate, offs, pos1, pos2, out):
@@ -170,7 +170,7 @@ def tile_routed_moe_kernel(tc, xT, w_words, w_scales, b, gate, offs, pos1, pos2,
             nc.tensor.matmul(both[:], ident[:], u[:], start=True, stop=False)
             nc.tensor.matmul(both[:], ident[:], v[:], start=False, stop=True)
             nc.scalar.copy(out=o[:], in_=both[:])
-            nc.sync.dma_start(out=out[:, t0 : t0 + n], in_=o[:])
+            nc.scalar.dma_start(out=out[:, t0 : t0 + n], in_=o[:])
             t0 += n
 
         rest = T - t0

@@ -6,6 +6,7 @@ from concourse.masks import make_identity
 K, T, E, C, N = 1024, 2048, 16, 256, 128
 P = 128
 PASSES = 2
+BANK = 512
 SLOTS = E * C
 FLOPS = 2 * SLOTS * K * N
 
@@ -24,8 +25,8 @@ CHUNKS = (
     ((512, 0, (512,)), (512, 0, (512,)), (512, 0, (512,)), (512, 0, (256, 256))),
 )
 WORD0_CUTS = (1536, 1536, 1024)
-LAST_GATHERS = ((1536, (1536,)), (1536, (1536,)), (1024, (512, 256, 256)))
-TENSOR_ADDS = (256, 512, 512, 256)
+LAST_GATHERS = (("scales", 1536), ("scales", 1536), ("words", 2048), ("words", 1536), ("scales", 1024), ("words", 256), ("words", 256))
+TENSOR_ADDS = (512, 1024)
 VECTOR_ADDS = (256, 256)
 
 
@@ -41,7 +42,8 @@ def tile_routed_moe_kernel(tc, xT, w_words, w_scales, b, gate, offs, pos1, pos2,
         pos2_sb = lists.tile([P, T // 16], U16, name="pos2_sb")
 
         grouped = [keep.tile([P, T, 4], BF16, name="grouped%d" % a, align_bytes=64) for a in range(PASSES)]
-        words = [keep.tile([P, T], U32, name="words%d" % a, align_bytes=64) for a in range(PASSES)]
+        both_words = keep.tile([P, PASSES * T], U32, name="both_words", align_bytes=64)
+        words = [both_words[:, T : 2 * T], both_words[:, 0:T]]
         scales = keep.tile([P, T], U8, name="scales", align_bytes=64)
         slot_words = [keep.tile([P, SLOTS], U32, name="slot_words%d" % a, align_bytes=64) for a in range(PASSES)]
         slot_scales = keep.tile([P, SLOTS], U8, name="slot_scales", align_bytes=64)
@@ -92,7 +94,8 @@ def tile_routed_moe_kernel(tc, xT, w_words, w_scales, b, gate, offs, pos1, pos2,
 
         def gather_words(a, s0, n):
             cols = slice(s0, s0 + n)
-            nc.vector.tensor_copy(slot_words[a][:, cols], words[a][:].indirect(offs_sb[:, s0 // 16 : (s0 + n) // 16]))
+            window = words[a] if n < T else both_words[:]
+            nc.vector.tensor_copy(slot_words[a][:, cols], window.indirect(offs_sb[:, s0 // 16 : (s0 + n) // 16]))
 
         def gather_scales(s0, n):
             cols = slice(s0, s0 + n)
@@ -142,16 +145,20 @@ def tile_routed_moe_kernel(tc, xT, w_words, w_scales, b, gate, offs, pos1, pos2,
             s0 += n
         for chunk in chunks1:
             quantise(1, chunk)
-        s0 = 0
-        for n_scales, word_cuts in LAST_GATHERS:
-            gather_scales(s0, n_scales)
-            for n in word_cuts:
-                gather_words(1, s0, n)
-                for e in range(s0 // C, (s0 + n) // C):
-                    step = C // 2 if e == E - 1 else C
-                    for lo in range(0, C, step):
-                        expert(e, lo, lo + step)
-                s0 += n
+        have = {"scales": 0, "words": 0}
+        done = 0
+        for sort, n in LAST_GATHERS:
+            if sort == "scales":
+                gather_scales(have[sort], n)
+            else:
+                gather_words(1, have[sort], n)
+            have[sort] += n
+            ready = min(have.values()) // C
+            for e in range(done, ready):
+                step = C // 2 if e == E - 1 else C
+                for lo in range(0, C, step):
+                    expert(e, lo, lo + step)
+            done = ready
 
         def shares(name, t0, n):
             return keep.tile([P, n], F32, name="%s%d" % (name, t0))
@@ -166,11 +173,13 @@ def tile_routed_moe_kernel(tc, xT, w_words, w_scales, b, gate, offs, pos1, pos2,
             u, v, o = shares("u", t0, n), shares("v", t0, n), shares("o", t0, n)
             weigh(u[:], 0, pos1_sb, t0, n)
             weigh(v[:], 1, pos2_sb, t0, n)
-            both = psum.tile([P, n], F32, name="both")
-            nc.tensor.matmul(both[:], ident[:], u[:], start=True, stop=False)
-            nc.tensor.matmul(both[:], ident[:], v[:], start=False, stop=True)
-            nc.scalar.copy(out=o[:], in_=both[:])
-            nc.scalar.dma_start(out=out[:, t0 : t0 + n], in_=o[:])
+            banks = [(slice(lo, lo + BANK), psum.tile([P, BANK], F32, name="both")) for lo in range(0, n, BANK)]
+            for cols, both in banks:
+                nc.tensor.matmul(both[:], ident[:], u[:, cols], start=True, stop=False)
+            for cols, both in banks:
+                nc.tensor.matmul(both[:], ident[:], v[:, cols], start=False, stop=True)
+                nc.scalar.copy(out=o[:, cols], in_=both[:])
+                nc.scalar.dma_start(out=out[:, t0 + cols.start : t0 + cols.stop], in_=o[:, cols])
             t0 += n
 
         rest = T - t0

@@ -5,9 +5,14 @@ from concourse.masks import make_identity
 
 K, T, E, C, N = 1024, 2048, 16, 256, 128
 P = 128
-PASSES = 2
-BANK = 512
+PACK = 4
+K_PASS = P * PACK
+PASSES = K // K_PASS
 SLOTS = E * C
+PER_COLUMN = 16
+QUADRANT = 32
+SCALE_ROWS = 4
+BANK = 512
 FLOPS = 2 * SLOTS * K * N
 
 F32 = mybir.dt.float32
@@ -20,14 +25,22 @@ FP8X4 = mybir.dt.float8_e4m3fn_x4
 MULT = mybir.AluOpType.mult
 SILU = mybir.ActivationFunctionType.Silu
 
-CHUNKS = (
-    ((768, 256, (256, 512)), (640, 320, (128, 512)), (384, 224, (128, 256)), (256, 176, (256,))),
+LOADS = (
+    ((768, 320, (256, 512)), (640, 352, (128, 512)), (384, 256, (256, 128)), (256, 160, (128, 128))),
     ((512, 0, (512,)), (512, 0, (512,)), (512, 0, (512,)), (512, 0, (256, 256))),
 )
-WORD0_CUTS = (1536, 1536, 1024)
-LAST_GATHERS = (("scales", 1536), ("scales", 1536), ("words", 2048), ("words", 1536), ("scales", 1024), ("words", 256), ("words", 256))
-TENSOR_ADDS = (512, 1024)
-VECTOR_ADDS = (256, 256)
+FIRST_GATHERS = (1536, 1536, 1024)
+LAST_GATHERS = (
+    ("scales", 1536),
+    ("scales", 1536),
+    ("words", 2048),
+    ("words", 1536),
+    ("scales", 1024),
+    ("words", 256),
+    ("words", 256),
+)
+TENSOR_ADDS = (384, 1024)
+VECTOR_ADDS = (320, 320)
 
 
 def tile_routed_moe_kernel(tc, xT, w_words, w_scales, b, gate, offs, pos1, pos2, out):
@@ -37,11 +50,11 @@ def tile_routed_moe_kernel(tc, xT, w_words, w_scales, b, gate, offs, pos1, pos2,
         keep = ctx.enter_context(tc.tile_pool(name="keep", bufs=1))
         psum = ctx.enter_context(tc.psum_pool(name="psum", bufs=4))
 
-        offs_sb = lists.tile([P, SLOTS // 16], U16, name="offs_sb")
-        pos1_sb = lists.tile([P, T // 16], U16, name="pos1_sb")
-        pos2_sb = lists.tile([P, T // 16], U16, name="pos2_sb")
+        offs_sb = lists.tile([P, SLOTS // PER_COLUMN], U16, name="offs_sb")
+        pos1_sb = lists.tile([P, T // PER_COLUMN], U16, name="pos1_sb")
+        pos2_sb = lists.tile([P, T // PER_COLUMN], U16, name="pos2_sb")
 
-        grouped = [keep.tile([P, T, 4], BF16, name="grouped%d" % a, align_bytes=64) for a in range(PASSES)]
+        grouped = [keep.tile([P, T, PACK], BF16, name="grouped%d" % a, align_bytes=64) for a in range(PASSES)]
         both_words = keep.tile([P, PASSES * T], U32, name="both_words", align_bytes=64)
         words = [both_words[:, T : 2 * T], both_words[:, 0:T]]
         scales = keep.tile([P, T], U8, name="scales", align_bytes=64)
@@ -52,22 +65,25 @@ def tile_routed_moe_kernel(tc, xT, w_words, w_scales, b, gate, offs, pos1, pos2,
         b_sb = keep.tile([P, E], F32, name="b_sb")
         gate_sb = [keep.tile([P, T], F32, name="gate_sb%d" % r) for r in range(2)]
         y = keep.tile([P, SLOTS], F32, name="y")
-
         ident = keep.tile([P, P], F32, name="ident")
+
         nc.vector.memset(scales[:].bitcast(I32), 0)
         nc.vector.memset(ws_sb[:].rearrange("p e n -> p (e n)").bitcast(I32), 0)
         make_identity(nc, ident[:])
 
+        def offsets(list_sb, first, n):
+            return list_sb[:, first // PER_COLUMN : (first + n) // PER_COLUMN]
+
         def load(a):
-            got = []
+            loaded = []
             t0 = 0
-            rows = xT[a * 512 : (a + 1) * 512, :].rearrange("(p j) t -> p j t", j=4)
-            for n, v, widths in CHUNKS[a]:
-                raw = keep.tile([P, 4, n], F32, name="raw%d_%d" % (a, t0))
+            rows = xT[a * K_PASS : (a + 1) * K_PASS, :].rearrange("(p j) t -> p j t", j=PACK)
+            for n, on_vector, widths in LOADS[a]:
+                raw = keep.tile([P, PACK, n], F32, name="raw%d_%d" % (a, t0))
                 nc.sync.dma_start(out=raw[:], in_=rows[:, :, t0 : t0 + n])
-                got.append((raw, t0, n, v, widths))
+                loaded.append((raw, t0, on_vector, widths))
                 t0 += n
-            return got
+            return loaded
 
         def interleave(copy, a, raw, t0, lo, hi):
             copy(
@@ -75,31 +91,29 @@ def tile_routed_moe_kernel(tc, xT, w_words, w_scales, b, gate, offs, pos1, pos2,
                 in_=raw[:, :, lo:hi].rearrange("p j (c i) -> p c j i", i=4),
             )
 
-        def quantise(a, chunk):
-            raw, t0, n, v, widths = chunk
+        def quantise(a, raw, t0, on_vector, widths):
             lo = 0
             for m in widths:
-                if lo + m > v:
-                    interleave(nc.scalar.copy, a, raw, t0, max(lo, v), lo + m)
+                if lo + m > on_vector:
+                    interleave(nc.scalar.copy, a, raw, t0, max(lo, on_vector), lo + m)
                 lo += m
-            if v:
-                interleave(nc.vector.tensor_copy, a, raw, t0, 0, v)
+            if on_vector:
+                interleave(nc.vector.tensor_copy, a, raw, t0, 0, on_vector)
+            lo = t0
             for m in widths:
                 nc.vector.quantize_mx(
-                    out=words[a][:, t0 : t0 + m].bitcast(FP8X4),
-                    scales=scales[4 * a : P, t0 : t0 + m],
-                    in_=grouped[a][:, t0 : t0 + m, :].rearrange("p t j -> p (t j)"),
+                    out=words[a][:, lo : lo + m].bitcast(FP8X4),
+                    scales=scales[SCALE_ROWS * a : P, lo : lo + m],
+                    in_=grouped[a][:, lo : lo + m, :].rearrange("p t j -> p (t j)"),
                 )
-                t0 += m
+                lo += m
 
         def gather_words(a, s0, n):
-            cols = slice(s0, s0 + n)
             window = words[a] if n < T else both_words[:]
-            nc.vector.tensor_copy(slot_words[a][:, cols], window.indirect(offs_sb[:, s0 // 16 : (s0 + n) // 16]))
+            nc.vector.tensor_copy(slot_words[a][:, s0 : s0 + n], window.indirect(offsets(offs_sb, s0, n)))
 
         def gather_scales(s0, n):
-            cols = slice(s0, s0 + n)
-            nc.vector.tensor_copy(slot_scales[:, cols], scales[:].indirect(offs_sb[:, s0 // 16 : (s0 + n) // 16]))
+            nc.vector.tensor_copy(slot_scales[:, s0 : s0 + n], scales[:].indirect(offsets(offs_sb, s0, n)))
 
         def expert(e, lo, hi):
             cols = slice(e * C + lo, e * C + hi)
@@ -108,28 +122,36 @@ def tile_routed_moe_kernel(tc, xT, w_words, w_scales, b, gate, offs, pos1, pos2,
                 nc.tensor.matmul_mx(
                     out=acc[:],
                     lhsT=w_sb[:, e, a, :].bitcast(FP8X4),
-                    lhsT_scale=ws_sb[4 * a : P, e, :],
+                    lhsT_scale=ws_sb[SCALE_ROWS * a : P, e, :],
                     rhs=slot_words[a][:, cols].bitcast(FP8X4),
-                    rhs_scale=slot_scales[4 * a : P, cols],
+                    rhs_scale=slot_scales[SCALE_ROWS * a : P, cols],
                     start=(a == 0),
                     stop=(a == PASSES - 1),
                 )
             nc.scalar.activation(out=y[:, cols], in_=acc[:], func=SILU, bias=b_sb[:, e : e + 1])
 
-        chunks0 = load(0)
+        def weigh(dst, r, pos_sb, t0, n):
+            nc.vector.tensor_tensor(dst, y[:].indirect(offsets(pos_sb, t0, n)), gate_sb[r][:, t0 : t0 + n], MULT)
+
+        def token_tile(name, t0, n):
+            return keep.tile([P, n], F32, name="%s%d" % (name, t0))
+
+        loads0 = load(0)
         nc.sync.dma_start(offs_sb[:], offs)
-        chunks1 = load(1)
+        loads1 = load(1)
         for a in range(PASSES):
-            for q in range(4):
+            for q in range(P // QUADRANT):
+                row = QUADRANT * q + SCALE_ROWS * a
+                blocks = slice(SCALE_ROWS * q, SCALE_ROWS * (q + 1))
                 nc.sync.dma_start(
-                    out=ws_sb[32 * q + 4 * a : 32 * q + 4 * a + 4, :, :].bitcast(I32),
-                    in_=w_scales[:, a, 4 * q : 4 * q + 4, :].rearrange("e q n -> q e n").bitcast(I32),
+                    out=ws_sb[row : row + SCALE_ROWS, :, :].bitcast(I32),
+                    in_=w_scales[:, a, blocks, :].rearrange("e q n -> q e n").bitcast(I32),
                 )
-        for h in range(2):
-            es = slice(h * E // 2, (h + 1) * E // 2)
+        for half in range(2):
+            experts = slice(half * E // 2, (half + 1) * E // 2)
             nc.sync.dma_start(
-                out=w_sb[:, es, :, :].rearrange("p e a n -> p (e a) n"),
-                in_=w_words[es].rearrange("e a p n r -> p (e a) (n r)").bitcast(I32),
+                out=w_sb[:, experts, :, :].rearrange("p e a n -> p (e a) n"),
+                in_=w_words[experts].rearrange("e a p n r -> p (e a) (n r)").bitcast(I32),
             )
         nc.sync.dma_start(b_sb[:], b)
         nc.sync.dma_start(pos1_sb[:], pos1)
@@ -137,60 +159,53 @@ def tile_routed_moe_kernel(tc, xT, w_words, w_scales, b, gate, offs, pos1, pos2,
         for r in range(2):
             nc.sync.dma_start(gate_sb[r][:], gate[r])
 
-        for chunk in chunks0:
-            quantise(0, chunk)
+        for loaded in loads0:
+            quantise(0, *loaded)
         s0 = 0
-        for n in WORD0_CUTS:
+        for n in FIRST_GATHERS:
             gather_words(0, s0, n)
             s0 += n
-        for chunk in chunks1:
-            quantise(1, chunk)
-        have = {"scales": 0, "words": 0}
-        done = 0
-        for sort, n in LAST_GATHERS:
-            if sort == "scales":
-                gather_scales(have[sort], n)
+        for loaded in loads1:
+            quantise(1, *loaded)
+        gathered = {"scales": 0, "words": 0}
+        started = 0
+        for what, n in LAST_GATHERS:
+            if what == "scales":
+                gather_scales(gathered[what], n)
             else:
-                gather_words(1, have[sort], n)
-            have[sort] += n
-            ready = min(have.values()) // C
-            for e in range(done, ready):
+                gather_words(1, gathered[what], n)
+            gathered[what] += n
+            ready = min(gathered.values()) // C
+            for e in range(started, ready):
                 step = C // 2 if e == E - 1 else C
                 for lo in range(0, C, step):
                     expert(e, lo, lo + step)
-            done = ready
-
-        def shares(name, t0, n):
-            return keep.tile([P, n], F32, name="%s%d" % (name, t0))
-
-        def weigh(dst, r, pos_sb, t0, n):
-            nc.vector.tensor_tensor(
-                dst, y[:].indirect(pos_sb[:, t0 // 16 : (t0 + n) // 16]), gate_sb[r][:, t0 : t0 + n], MULT
-            )
+            started = ready
 
         t0 = 0
         for n in TENSOR_ADDS:
-            u, v, o = shares("u", t0, n), shares("v", t0, n), shares("o", t0, n)
-            weigh(u[:], 0, pos1_sb, t0, n)
-            weigh(v[:], 1, pos2_sb, t0, n)
-            banks = [(slice(lo, lo + BANK), psum.tile([P, BANK], F32, name="both")) for lo in range(0, n, BANK)]
-            for cols, both in banks:
-                nc.tensor.matmul(both[:], ident[:], u[:, cols], start=True, stop=False)
-            for cols, both in banks:
-                nc.tensor.matmul(both[:], ident[:], v[:, cols], start=False, stop=True)
-                nc.scalar.copy(out=o[:, cols], in_=both[:])
-                nc.scalar.dma_start(out=out[:, t0 + cols.start : t0 + cols.stop], in_=o[:, cols])
+            first, second, total = token_tile("first", t0, n), token_tile("second", t0, n), token_tile("total", t0, n)
+            weigh(first[:], 0, pos1_sb, t0, n)
+            weigh(second[:], 1, pos2_sb, t0, n)
+            width = min(n, BANK)
+            banks = [(slice(lo, lo + width), psum.tile([P, width], F32, name="pair")) for lo in range(0, n, width)]
+            for cols, pair in banks:
+                nc.tensor.matmul(pair[:], ident[:], first[:, cols], start=True, stop=False)
+            for cols, pair in banks:
+                nc.tensor.matmul(pair[:], ident[:], second[:, cols], start=False, stop=True)
+                nc.scalar.copy(out=total[:, cols], in_=pair[:])
+                nc.scalar.dma_start(out=out[:, t0 + cols.start : t0 + cols.stop], in_=total[:, cols])
             t0 += n
 
         rest = T - t0
-        u, v, o = shares("u", t0, rest), shares("v", t0, rest), shares("o", t0, rest)
-        weigh(u[:], 0, pos1_sb, t0, rest)
+        first, second, total = token_tile("first", t0, rest), token_tile("second", t0, rest), token_tile("total", t0, rest)
+        weigh(first[:], 0, pos1_sb, t0, rest)
         pieces = []
         lo = 0
         for n in VECTOR_ADDS:
             pieces.append(slice(lo, lo + n))
-            weigh(v[:, lo : lo + n], 1, pos2_sb, t0 + lo, n)
+            weigh(second[:, lo : lo + n], 1, pos2_sb, t0 + lo, n)
             lo += n
         for cols in pieces:
-            nc.vector.tensor_add(out=o[:, cols], in0=u[:, cols], in1=v[:, cols])
-            nc.sync.dma_start(out=out[:, t0 + cols.start : t0 + cols.stop], in_=o[:, cols])
+            nc.vector.tensor_add(out=total[:, cols], in0=first[:, cols], in1=second[:, cols])
+            nc.sync.dma_start(out=out[:, t0 + cols.start : t0 + cols.stop], in_=total[:, cols])

@@ -13,6 +13,7 @@ PER_COLUMN = 16
 QUADRANT = 32
 SCALE_ROWS = 4
 BANK = 512
+ALIGN = 256
 FLOPS = 2 * SLOTS * K * N
 
 F32 = mybir.dt.float32
@@ -27,9 +28,10 @@ SILU = mybir.ActivationFunctionType.Silu
 
 LOADS = (
     ((768, 320, (256, 512)), (640, 352, (128, 512)), (384, 256, (256, 128)), (256, 160, (128, 128))),
-    ((512, 0, (512,)), (512, 0, (512,)), (512, 0, (512,)), (512, 0, (256, 256))),
+    ((256, 0, (256,)), (512, 0, (512,)), (512, 0, (512,)), (512, 0, (512,)), (256, 0, (256,))),
 )
-FIRST_GATHERS = (1536, 1536, 1024)
+FIRST_GATHERS = (1536, 1536, 768)
+HELD_BACK = SLOTS - sum(FIRST_GATHERS)
 LAST_GATHERS = (
     ("scales", 1536),
     ("scales", 1536),
@@ -54,18 +56,18 @@ def tile_routed_moe_kernel(tc, xT, w_words, w_scales, b, gate, offs, pos1, pos2,
         pos1_sb = lists.tile([P, T // PER_COLUMN], U16, name="pos1_sb")
         pos2_sb = lists.tile([P, T // PER_COLUMN], U16, name="pos2_sb")
 
-        grouped = [keep.tile([P, T, PACK], BF16, name="grouped%d" % a, align_bytes=64) for a in range(PASSES)]
-        both_words = keep.tile([P, PASSES * T], U32, name="both_words", align_bytes=64)
+        grouped = [keep.tile([P, T, PACK], BF16, name="grouped%d" % a, align_bytes=ALIGN) for a in range(PASSES)]
+        both_words = keep.tile([P, PASSES * T], U32, name="both_words", align_bytes=ALIGN)
         words = [both_words[:, T : 2 * T], both_words[:, 0:T]]
-        scales = keep.tile([P, T], U8, name="scales", align_bytes=64)
-        slot_words = [keep.tile([P, SLOTS], U32, name="slot_words%d" % a, align_bytes=64) for a in range(PASSES)]
-        slot_scales = keep.tile([P, SLOTS], U8, name="slot_scales", align_bytes=64)
-        w_sb = keep.tile([P, E, PASSES, N], I32, name="w_sb", align_bytes=64)
-        ws_sb = keep.tile([P, E, N], U8, name="ws_sb", align_bytes=64)
+        scales = keep.tile([P, T], U8, name="scales", align_bytes=ALIGN)
+        slot_words = [keep.tile([P, SLOTS], U32, name="slot_words%d" % a, align_bytes=ALIGN) for a in range(PASSES)]
+        slot_scales = keep.tile([P, SLOTS], U8, name="slot_scales", align_bytes=ALIGN)
+        w_sb = keep.tile([P, E, PASSES, N], I32, name="w_sb", align_bytes=ALIGN)
+        ws_sb = keep.tile([P, E, N], U8, name="ws_sb", align_bytes=ALIGN)
         b_sb = keep.tile([P, E], F32, name="b_sb")
-        gate_sb = [keep.tile([P, T], F32, name="gate_sb%d" % r) for r in range(2)]
-        y = keep.tile([P, SLOTS], F32, name="y")
-        ident = keep.tile([P, P], F32, name="ident")
+        gate_sb = [keep.tile([P, T], F32, name="gate_sb%d" % r, align_bytes=ALIGN) for r in range(2)]
+        y = keep.tile([P, SLOTS], F32, name="y", align_bytes=ALIGN)
+        ident = keep.tile([P, P], F32, name="ident", align_bytes=ALIGN)
 
         nc.vector.memset(scales[:].bitcast(I32), 0)
         nc.vector.memset(ws_sb[:].rearrange("p e n -> p (e n)").bitcast(I32), 0)
@@ -79,7 +81,7 @@ def tile_routed_moe_kernel(tc, xT, w_words, w_scales, b, gate, offs, pos1, pos2,
             t0 = 0
             rows = xT[a * K_PASS : (a + 1) * K_PASS, :].rearrange("(p j) t -> p j t", j=PACK)
             for n, on_vector, widths in LOADS[a]:
-                raw = keep.tile([P, PACK, n], F32, name="raw%d_%d" % (a, t0))
+                raw = keep.tile([P, PACK, n], F32, name="raw%d_%d" % (a, t0), align_bytes=ALIGN)
                 nc.sync.dma_start(out=raw[:], in_=rows[:, :, t0 : t0 + n])
                 loaded.append((raw, t0, on_vector, widths))
                 t0 += n
@@ -134,7 +136,7 @@ def tile_routed_moe_kernel(tc, xT, w_words, w_scales, b, gate, offs, pos1, pos2,
             nc.vector.tensor_tensor(dst, y[:].indirect(offsets(pos_sb, t0, n)), gate_sb[r][:, t0 : t0 + n], MULT)
 
         def token_tile(name, t0, n):
-            return keep.tile([P, n], F32, name="%s%d" % (name, t0))
+            return keep.tile([P, n], F32, name="%s%d" % (name, t0), align_bytes=ALIGN)
 
         loads0 = load(0)
         nc.sync.dma_start(offs_sb[:], offs)
@@ -167,6 +169,7 @@ def tile_routed_moe_kernel(tc, xT, w_words, w_scales, b, gate, offs, pos1, pos2,
             s0 += n
         for loaded in loads1:
             quantise(1, *loaded)
+        gather_words(0, s0, HELD_BACK)
         gathered = {"scales": 0, "words": 0}
         started = 0
         for what, n in LAST_GATHERS:

@@ -27,7 +27,7 @@ MULT = mybir.AluOpType.mult
 SILU = mybir.ActivationFunctionType.Silu
 
 LOADS = (
-    ((768, 320, (256, 512)), (640, 352, (128, 512)), (384, 256, (256, 128)), (256, 160, (128, 128))),
+    ((512, 128, (512,)), (512, 192, (512,)), (512, 320, (256, 256)), (256, 160, (128, 128)), (256, 160, (128, 128))),
     ((256, 0, (256,)), (512, 0, (512,)), (512, 0, (512,)), (512, 0, (512,)), (256, 0, (256,))),
 )
 FIRST_GATHERS = (1536, 1536, 768)

@@ -27,7 +27,7 @@ MULT = mybir.AluOpType.mult
 SILU = mybir.ActivationFunctionType.Silu
 
 LOADS = (
-    ((512, 128, (512,)), (512, 192, (512,)), (512, 320, (256, 256)), (256, 160, (128, 128)), (256, 160, (128, 128))),
+    ((512, 128, (512,)), (512, 256, (256, 256)), (256, 128, (128, 128)), (256, 128, (128, 128)), (256, 128, (128, 128)), (256, 160, (128, 128))),
     ((256, 0, (256,)), (512, 0, (512,)), (512, 0, (512,)), (512, 0, (512,)), (256, 0, (256,))),
 )
 FIRST_GATHERS = (1536, 1536, 768)

@@ -1,4 +1,5 @@
 from contextlib import ExitStack
+from itertools import accumulate
 
 import concourse.mybir as mybir
 from concourse.masks import make_identity
@@ -12,6 +13,7 @@ SLOTS = E * C
 PER_COLUMN = 16
 QUADRANT = 32
 SCALE_ROWS = 4
+SCALE_ROW = (SCALE_ROWS, 0)
 BANK = 512
 ALIGN = 256
 FLOPS = 2 * SLOTS * K * N
@@ -28,7 +30,7 @@ SILU = mybir.ActivationFunctionType.Silu
 
 LOADS = (
     ((512, 128, (512,)), (512, 256, (256, 256)), (256, 128, (128, 128)), (256, 128, (128, 128)), (256, 128, (128, 128)), (256, 160, (128, 128))),
-    ((256, 0, (256,)), (512, 0, (512,)), (512, 0, (512,)), (512, 0, (512,)), (256, 0, (256,))),
+    ((256, 0, ()), (512, 0, ()), (512, 0, (1024,)), (512, 0, (512,)), (256, 0, (256, 256))),
 )
 FIRST_GATHERS = (1536, 1536, 768)
 HELD_BACK = SLOTS - sum(FIRST_GATHERS)
@@ -41,8 +43,9 @@ LAST_GATHERS = (
     ("words", 256),
     ("words", 256),
 )
-TENSOR_ADDS = (384, 1024)
-VECTOR_ADDS = (320, 320)
+TENSOR_ADDS = (384, 512, 384)
+VECTOR_ADDS = (384, 384)
+COMBINE_GATHERS = ((0, 384), (1, 896), (0, 1280), (1, 1664), (0, 2048), (1, 2048))
 
 
 def tile_routed_moe_kernel(tc, xT, w_words, w_scales, b, gate, offs, pos1, pos2, out):
@@ -60,7 +63,8 @@ def tile_routed_moe_kernel(tc, xT, w_words, w_scales, b, gate, offs, pos1, pos2,
         both_words = keep.tile([P, PASSES * T], U32, name="both_words", align_bytes=ALIGN)
         words = [both_words[:, T : 2 * T], both_words[:, 0:T]]
         scales = keep.tile([P, T], U8, name="scales", align_bytes=ALIGN)
-        slot_words = [keep.tile([P, SLOTS], U32, name="slot_words%d" % a, align_bytes=ALIGN) for a in range(PASSES)]
+        slot_words = [keep.tile([P, SLOTS - HELD_BACK * (1 - a)], U32, name="slot_words%d" % a, align_bytes=ALIGN) for a in range(PASSES)]
+        held_words = []
         slot_scales = keep.tile([P, SLOTS], U8, name="slot_scales", align_bytes=ALIGN)
         w_sb = keep.tile([P, E, PASSES, N], I32, name="w_sb", align_bytes=ALIGN)
         ws_sb = keep.tile([P, E, N], U8, name="ws_sb", align_bytes=ALIGN)
@@ -83,7 +87,7 @@ def tile_routed_moe_kernel(tc, xT, w_words, w_scales, b, gate, offs, pos1, pos2,
             for n, on_vector, widths in LOADS[a]:
                 raw = keep.tile([P, PACK, n], F32, name="raw%d_%d" % (a, t0), align_bytes=ALIGN)
                 nc.sync.dma_start(out=raw[:], in_=rows[:, :, t0 : t0 + n])
-                loaded.append((raw, t0, on_vector, widths))
+                loaded.append((raw, t0, n, on_vector, widths))
                 t0 += n
             return loaded
 
@@ -93,26 +97,31 @@ def tile_routed_moe_kernel(tc, xT, w_words, w_scales, b, gate, offs, pos1, pos2,
                 in_=raw[:, :, lo:hi].rearrange("p j (c i) -> p c j i", i=4),
             )
 
-        def quantise(a, raw, t0, on_vector, widths):
-            lo = 0
-            for m in widths:
-                if lo + m > on_vector:
-                    interleave(nc.scalar.copy, a, raw, t0, max(lo, on_vector), lo + m)
-                lo += m
+        quantised = [0] * PASSES
+
+        def quantise(a, raw, t0, n, on_vector, widths):
+            cuts = [c - t0 for c in accumulate(widths, initial=quantised[a]) if t0 + on_vector < c < t0 + n]
+            for lo, hi in zip([on_vector] + cuts, cuts + [n]):
+                interleave(nc.scalar.copy, a, raw, t0, lo, hi)
             if on_vector:
                 interleave(nc.vector.tensor_copy, a, raw, t0, 0, on_vector)
-            lo = t0
             for m in widths:
+                lo = quantised[a]
                 nc.vector.quantize_mx(
                     out=words[a][:, lo : lo + m].bitcast(FP8X4),
-                    scales=scales[SCALE_ROWS * a : P, lo : lo + m],
+                    scales=scales[SCALE_ROW[a] : P, lo : lo + m],
                     in_=grouped[a][:, lo : lo + m, :].rearrange("p t j -> p (t j)"),
                 )
-                lo += m
+                quantised[a] = lo + m
+
+        def slots_of(a, cols):
+            if a == 0 and cols.start >= SLOTS - HELD_BACK:
+                return held_words[0][:, cols.start - (SLOTS - HELD_BACK) : cols.stop - (SLOTS - HELD_BACK)]
+            return slot_words[a][:, cols]
 
         def gather_words(a, s0, n):
             window = words[a] if n < T else both_words[:]
-            nc.vector.tensor_copy(slot_words[a][:, s0 : s0 + n], window.indirect(offsets(offs_sb, s0, n)))
+            nc.vector.tensor_copy(slots_of(a, slice(s0, s0 + n)), window.indirect(offsets(offs_sb, s0, n)))
 
         def gather_scales(s0, n):
             nc.vector.tensor_copy(slot_scales[:, s0 : s0 + n], scales[:].indirect(offsets(offs_sb, s0, n)))
@@ -124,9 +133,9 @@ def tile_routed_moe_kernel(tc, xT, w_words, w_scales, b, gate, offs, pos1, pos2,
                 nc.tensor.matmul_mx(
                     out=acc[:],
                     lhsT=w_sb[:, e, a, :].bitcast(FP8X4),
-                    lhsT_scale=ws_sb[SCALE_ROWS * a : P, e, :],
-                    rhs=slot_words[a][:, cols].bitcast(FP8X4),
-                    rhs_scale=slot_scales[SCALE_ROWS * a : P, cols],
+                    lhsT_scale=ws_sb[SCALE_ROW[a] : P, e, :],
+                    rhs=slots_of(a, cols).bitcast(FP8X4),
+                    rhs_scale=slot_scales[SCALE_ROW[a] : P, cols],
                     start=(a == 0),
                     stop=(a == PASSES - 1),
                 )
@@ -135,15 +144,12 @@ def tile_routed_moe_kernel(tc, xT, w_words, w_scales, b, gate, offs, pos1, pos2,
         def weigh(dst, r, pos_sb, t0, n):
             nc.vector.tensor_tensor(dst, y[:].indirect(offsets(pos_sb, t0, n)), gate_sb[r][:, t0 : t0 + n], MULT)
 
-        def token_tile(name, t0, n):
-            return keep.tile([P, n], F32, name="%s%d" % (name, t0), align_bytes=ALIGN)
-
         loads0 = load(0)
         nc.sync.dma_start(offs_sb[:], offs)
         loads1 = load(1)
         for a in range(PASSES):
             for q in range(P // QUADRANT):
-                row = QUADRANT * q + SCALE_ROWS * a
+                row = QUADRANT * q + SCALE_ROW[a]
                 blocks = slice(SCALE_ROWS * q, SCALE_ROWS * (q + 1))
                 nc.sync.dma_start(
                     out=ws_sb[row : row + SCALE_ROWS, :, :].bitcast(I32),
@@ -158,8 +164,10 @@ def tile_routed_moe_kernel(tc, xT, w_words, w_scales, b, gate, offs, pos1, pos2,
         nc.sync.dma_start(b_sb[:], b)
         nc.sync.dma_start(pos1_sb[:], pos1)
         nc.sync.dma_start(pos2_sb[:], pos2)
-        for r in range(2):
-            nc.sync.dma_start(gate_sb[r][:], gate[r])
+        reached = [0, 0]
+        for r, end in COMBINE_GATHERS:
+            nc.sync.dma_start(gate_sb[r][:, reached[r] : end], gate[r][:, reached[r] : end])
+            reached[r] = end
 
         for loaded in loads0:
             quantise(0, *loaded)
@@ -169,6 +177,7 @@ def tile_routed_moe_kernel(tc, xT, w_words, w_scales, b, gate, offs, pos1, pos2,
             s0 += n
         for loaded in loads1:
             quantise(1, *loaded)
+        held_words.append(keep.tile([P, HELD_BACK], U32, name="raw1_%d" % loads1[-1][1], align_bytes=ALIGN))
         gather_words(0, s0, HELD_BACK)
         gathered = {"scales": 0, "words": 0}
         started = 0
@@ -185,30 +194,42 @@ def tile_routed_moe_kernel(tc, xT, w_words, w_scales, b, gate, offs, pos1, pos2,
                     expert(e, lo, lo + step)
             started = ready
 
-        t0 = 0
-        for n in TENSOR_ADDS:
-            first, second, total = token_tile("first", t0, n), token_tile("second", t0, n), token_tile("total", t0, n)
-            weigh(first[:], 0, pos1_sb, t0, n)
-            weigh(second[:], 1, pos2_sb, t0, n)
-            width = min(n, BANK)
-            banks = [(slice(lo, lo + width), psum.tile([P, width], F32, name="pair")) for lo in range(0, n, width)]
-            for cols, pair in banks:
-                nc.tensor.matmul(pair[:], ident[:], first[:, cols], start=True, stop=False)
-            for cols, pair in banks:
-                nc.tensor.matmul(pair[:], ident[:], second[:, cols], start=False, stop=True)
-                nc.scalar.copy(out=total[:, cols], in_=pair[:])
-                nc.scalar.dma_start(out=out[:, t0 + cols.start : t0 + cols.stop], in_=total[:, cols])
-            t0 += n
+        shares = [[], []]
 
-        rest = T - t0
-        first, second, total = token_tile("first", t0, rest), token_tile("second", t0, rest), token_tile("total", t0, rest)
-        weigh(first[:], 0, pos1_sb, t0, rest)
+        def share(r, cols):
+            begin, tile = [(b, t) for b, e, t in shares[r] if b <= cols.start and cols.stop <= e][0]
+            return tile[:, cols.start - begin : cols.stop - begin]
+
+        def total(cols):
+            return keep.tile([P, cols.stop - cols.start], F32, name="total%d" % cols.start, align_bytes=ALIGN)
+
+        pos_sb = (pos1_sb, pos2_sb)
         pieces = []
-        lo = 0
-        for n in VECTOR_ADDS:
-            pieces.append(slice(lo, lo + n))
-            weigh(second[:, lo : lo + n], 1, pos2_sb, t0 + lo, n)
-            lo += n
-        for cols in pieces:
-            nc.vector.tensor_add(out=total[:, cols], in0=first[:, cols], in1=second[:, cols])
-            nc.sync.dma_start(out=out[:, t0 + cols.start : t0 + cols.stop], in_=total[:, cols])
+        t0 = 0
+        for n in TENSOR_ADDS + VECTOR_ADDS:
+            pieces.append(slice(t0, t0 + n))
+            t0 += n
+        on_tensor = pieces[: len(TENSOR_ADDS)]
+        banks = {}
+        reached = [0, 0]
+        for r, end in COMBINE_GATHERS:
+            begin = reached[r]
+            weighed = keep.tile([P, end - begin], F32, name="share%d_%d" % (r, begin), align_bytes=ALIGN)
+            weigh(weighed[:], r, pos_sb[r], begin, end - begin)
+            shares[r].append((begin, end, weighed))
+            reached[r] = end
+            for cols in on_tensor:
+                if begin < cols.stop <= end:
+                    first = cols.start not in banks
+                    if first:
+                        banks[cols.start] = psum.tile([P, cols.stop - cols.start], F32, name="pair")
+                    pair = banks[cols.start]
+                    nc.tensor.matmul(pair[:], ident[:], share(r, cols), start=first, stop=not first)
+                    if not first:
+                        summed = total(cols)
+                        nc.scalar.copy(out=summed[:], in_=pair[:])
+                        nc.scalar.dma_start(out=out[:, cols], in_=summed[:])
+        for cols in pieces[len(TENSOR_ADDS) :]:
+            summed = total(cols)
+            nc.vector.tensor_add(out=summed[:], in0=share(0, cols), in1=share(1, cols))
+            nc.sync.dma_start(out=out[:, cols], in_=summed[:])

@@ -30,9 +30,9 @@ SILU = mybir.ActivationFunctionType.Silu
 
 LOADS = (
     ((512, 128, (512,)), (512, 256, (256, 256)), (256, 128, (128, 128)), (256, 128, (128, 128)), (256, 128, (128, 128)), (256, 160, (128, 128))),
-    ((256, 0, ()), (512, 0, ()), (512, 0, (1024,)), (512, 0, (512,)), (256, 0, (256, 256))),
+    ((256, 0, ()), (512, 0, ()), (512, 0, (1024,)), (256, 0, (512,)), (256, 0, (256,)), (256, 0, (256,))),
 )
-FIRST_GATHERS = (1536, 1536, 768)
+FIRST_GATHERS = (1536, 1536, 640)
 HELD_BACK = SLOTS - sum(FIRST_GATHERS)
 LAST_GATHERS = (
     ("scales", 1536),
@@ -115,9 +115,11 @@ def tile_routed_moe_kernel(tc, xT, w_words, w_scales, b, gate, offs, pos1, pos2,
                 quantised[a] = lo + m
 
         def slots_of(a, cols):
-            if a == 0 and cols.start >= SLOTS - HELD_BACK:
-                return held_words[0][:, cols.start - (SLOTS - HELD_BACK) : cols.stop - (SLOTS - HELD_BACK)]
-            return slot_words[a][:, cols]
+            if a == 1:
+                return slot_words[a][:, cols]
+            if cols.start < HELD_BACK:
+                return held_words[0][:, cols]
+            return slot_words[a][:, cols.start - HELD_BACK : cols.stop - HELD_BACK]
 
         def gather_words(a, s0, n):
             window = words[a] if n < T else both_words[:]
@@ -171,14 +173,14 @@ def tile_routed_moe_kernel(tc, xT, w_words, w_scales, b, gate, offs, pos1, pos2,
 
         for loaded in loads0:
             quantise(0, *loaded)
-        s0 = 0
+        s0 = HELD_BACK
         for n in FIRST_GATHERS:
             gather_words(0, s0, n)
             s0 += n
         for loaded in loads1:
             quantise(1, *loaded)
         held_words.append(keep.tile([P, HELD_BACK], U32, name="raw1_%d" % loads1[-1][1], align_bytes=ALIGN))
-        gather_words(0, s0, HELD_BACK)
+        gather_words(0, 0, HELD_BACK)
         gathered = {"scales": 0, "words": 0}
         started = 0
         for what, n in LAST_GATHERS:
@@ -189,7 +191,7 @@ def tile_routed_moe_kernel(tc, xT, w_words, w_scales, b, gate, offs, pos1, pos2,
             gathered[what] += n
             ready = min(gathered.values()) // C
             for e in range(started, ready):
-                step = C // 2 if e == E - 1 else C
+                step = C // 2 if e in (HELD_BACK // C, E - 1) else C
                 for lo in range(0, C, step):
                     expert(e, lo, lo + step)
             started = ready

@@ -2,7 +2,6 @@ from contextlib import ExitStack
 from itertools import accumulate
 
 import concourse.mybir as mybir
-from concourse.masks import make_identity
 
 K, T, E, C, N = 1024, 2048, 16, 256, 128
 P = 128
@@ -14,7 +13,6 @@ PER_COLUMN = 16
 QUADRANT = 32
 SCALE_ROWS = 4
 SCALE_ROW = (SCALE_ROWS, 0)
-BANK = 512
 ALIGN = 256
 FLOPS = 2 * SLOTS * K * N
 
@@ -27,6 +25,7 @@ U8 = mybir.dt.uint8
 FP8X4 = mybir.dt.float8_e4m3fn_x4
 MULT = mybir.AluOpType.mult
 SILU = mybir.ActivationFunctionType.Silu
+COPY = mybir.ActivationFunctionType.Copy
 
 LOADS = (
     ((512, 128, (512,)), (512, 256, (256, 256)), (256, 128, (128, 128)), (256, 128, (128, 128)), (256, 128, (128, 128)), (256, 160, (128, 128))),
@@ -43,9 +42,8 @@ LAST_GATHERS = (
     ("words", 256),
     ("words", 256),
 )
-TENSOR_ADDS = (384, 512, 384)
-VECTOR_ADDS = (384, 384)
-COMBINE_GATHERS = ((0, 384), (1, 896), (0, 1280), (1, 1664), (0, 2048), (1, 2048))
+PIECES = ((576, True), (576, True), (384, False), (320, False), (192, False))
+ON_VECTOR = sum(n for n, on_vector in PIECES if on_vector)
 
 
 def tile_routed_moe_kernel(tc, xT, w_words, w_scales, b, gate, offs, pos1, pos2, out):
@@ -69,13 +67,11 @@ def tile_routed_moe_kernel(tc, xT, w_words, w_scales, b, gate, offs, pos1, pos2,
         w_sb = keep.tile([P, E, PASSES, N], I32, name="w_sb", align_bytes=ALIGN)
         ws_sb = keep.tile([P, E, N], U8, name="ws_sb", align_bytes=ALIGN)
         b_sb = keep.tile([P, E], F32, name="b_sb")
-        gate_sb = [keep.tile([P, T], F32, name="gate_sb%d" % r, align_bytes=ALIGN) for r in range(2)]
+        gate_sb = keep.tile([P, 2, T], F32, name="gate_sb", align_bytes=ALIGN)
         y = keep.tile([P, SLOTS], F32, name="y", align_bytes=ALIGN)
-        ident = keep.tile([P, P], F32, name="ident", align_bytes=ALIGN)
 
         nc.vector.memset(scales[:].bitcast(I32), 0)
         nc.vector.memset(ws_sb[:].rearrange("p e n -> p (e n)").bitcast(I32), 0)
-        make_identity(nc, ident[:])
 
         def offsets(list_sb, first, n):
             return list_sb[:, first // PER_COLUMN : (first + n) // PER_COLUMN]
@@ -143,9 +139,6 @@ def tile_routed_moe_kernel(tc, xT, w_words, w_scales, b, gate, offs, pos1, pos2,
                 )
             nc.scalar.activation(out=y[:, cols], in_=acc[:], func=SILU, bias=b_sb[:, e : e + 1])
 
-        def weigh(dst, r, pos_sb, t0, n):
-            nc.vector.tensor_tensor(dst, y[:].indirect(offsets(pos_sb, t0, n)), gate_sb[r][:, t0 : t0 + n], MULT)
-
         loads0 = load(0)
         nc.sync.dma_start(offs_sb[:], offs)
         loads1 = load(1)
@@ -157,19 +150,19 @@ def tile_routed_moe_kernel(tc, xT, w_words, w_scales, b, gate, offs, pos1, pos2,
                     out=ws_sb[row : row + SCALE_ROWS, :, :].bitcast(I32),
                     in_=w_scales[:, a, blocks, :].rearrange("e q n -> q e n").bitcast(I32),
                 )
-        for half in range(2):
+        def load_weights(half):
             experts = slice(half * E // 2, (half + 1) * E // 2)
             nc.sync.dma_start(
                 out=w_sb[:, experts, :, :].rearrange("p e a n -> p (e a) n"),
                 in_=w_words[experts].rearrange("e a p n r -> p (e a) (n r)").bitcast(I32),
             )
+
+        load_weights(0)
         nc.sync.dma_start(b_sb[:], b)
         nc.sync.dma_start(pos1_sb[:], pos1)
         nc.sync.dma_start(pos2_sb[:], pos2)
-        reached = [0, 0]
-        for r, end in COMBINE_GATHERS:
-            nc.sync.dma_start(gate_sb[r][:, reached[r] : end], gate[r][:, reached[r] : end])
-            reached[r] = end
+        nc.sync.dma_start(gate_sb[:], gate.rearrange("r p t -> p r t"))
+        load_weights(1)
 
         for loaded in loads0:
             quantise(0, *loaded)
@@ -196,42 +189,30 @@ def tile_routed_moe_kernel(tc, xT, w_words, w_scales, b, gate, offs, pos1, pos2,
                     expert(e, lo, lo + step)
             started = ready
 
-        shares = [[], []]
-
-        def share(r, cols):
-            begin, tile = [(b, t) for b, e, t in shares[r] if b <= cols.start and cols.stop <= e][0]
-            return tile[:, cols.start - begin : cols.stop - begin]
-
-        def total(cols):
-            return keep.tile([P, cols.stop - cols.start], F32, name="total%d" % cols.start, align_bytes=ALIGN)
-
         pos_sb = (pos1_sb, pos2_sb)
-        pieces = []
+
+        def results(r, t0, n):
+            return y[:].indirect(offsets(pos_sb[r], t0, n))
+
+        first = keep.tile([P, ON_VECTOR], F32, name="first", align_bytes=ALIGN)
+        nc.vector.tensor_tensor(first[:], results(0, 0, ON_VECTOR), gate_sb[:, 0, 0:ON_VECTOR], MULT)
+
+        def add(t0, n, weighed):
+            summed = keep.tile([P, n], F32, name="total%d" % t0, align_bytes=ALIGN)
+            other = first[:, t0 : t0 + n] if t0 < ON_VECTOR else weighed[:, 1, :]
+            nc.vector.tensor_add(out=summed[:], in0=weighed[:, 0, :], in1=other)
+            nc.sync.dma_start(out=out[:, t0 : t0 + n], in_=summed[:])
+
         t0 = 0
-        for n in TENSOR_ADDS + VECTOR_ADDS:
-            pieces.append(slice(t0, t0 + n))
+        waiting = None
+        for n, on_vector in PIECES:
+            r0 = int(on_vector)
+            plain = keep.tile([P, 2 - r0, n], F32, name="plain%d" % t0, align_bytes=ALIGN)
+            for r in range(r0, 2):
+                nc.scalar.activation(out=plain[:, r - r0, :], in_=results(r, t0, n), func=COPY)
+            nc.vector.tensor_tensor(plain[:], plain[:], gate_sb[:, r0:2, t0 : t0 + n], MULT)
+            if waiting:
+                add(*waiting)
+            waiting = (t0, n, plain)
             t0 += n
-        on_tensor = pieces[: len(TENSOR_ADDS)]
-        banks = {}
-        reached = [0, 0]
-        for r, end in COMBINE_GATHERS:
-            begin = reached[r]
-            weighed = keep.tile([P, end - begin], F32, name="share%d_%d" % (r, begin), align_bytes=ALIGN)
-            weigh(weighed[:], r, pos_sb[r], begin, end - begin)
-            shares[r].append((begin, end, weighed))
-            reached[r] = end
-            for cols in on_tensor:
-                if begin < cols.stop <= end:
-                    first = cols.start not in banks
-                    if first:
-                        banks[cols.start] = psum.tile([P, cols.stop - cols.start], F32, name="pair")
-                    pair = banks[cols.start]
-                    nc.tensor.matmul(pair[:], ident[:], share(r, cols), start=first, stop=not first)
-                    if not first:
-                        summed = total(cols)
-                        nc.scalar.copy(out=summed[:], in_=pair[:])
-                        nc.scalar.dma_start(out=out[:, cols], in_=summed[:])
-        for cols in pieces[len(TENSOR_ADDS) :]:
-            summed = total(cols)
-            nc.vector.tensor_add(out=summed[:], in0=share(0, cols), in1=share(1, cols))
-            nc.sync.dma_start(out=out[:, cols], in_=summed[:])
+        add(*waiting)

@@ -42,7 +42,7 @@ LAST_GATHERS = (
     ("words", 256),
     ("words", 256),
 )
-PIECES = ((576, True), (576, True), (384, False), (320, False), (192, False))
+PIECES = ((640, True), (640, True), (320, False), (256, False), (192, False))
 ON_VECTOR = sum(n for n, on_vector in PIECES if on_vector)
 
 
@@ -203,10 +203,11 @@ def tile_routed_moe_kernel(tc, xT, w_words, w_scales, b, gate, offs, pos1, pos2,
             nc.vector.tensor_add(out=summed[:], in0=weighed[:, 0, :], in1=other)
             nc.sync.dma_start(out=out[:, t0 : t0 + n], in_=summed[:])
 
-        t0 = 0
+        reached = [ON_VECTOR, 0]
         waiting = None
         for n, on_vector in PIECES:
             r0 = int(on_vector)
+            t0 = reached[r0]
             plain = keep.tile([P, 2 - r0, n], F32, name="plain%d" % t0, align_bytes=ALIGN)
             for r in range(r0, 2):
                 nc.scalar.activation(out=plain[:, r - r0, :], in_=results(r, t0, n), func=COPY)
@@ -214,5 +215,5 @@ def tile_routed_moe_kernel(tc, xT, w_words, w_scales, b, gate, offs, pos1, pos2,
             if waiting:
                 add(*waiting)
             waiting = (t0, n, plain)
-            t0 += n
+            reached[r0] += n
         add(*waiting)

@@ -31,7 +31,8 @@ LOADS = (
     ((512, 128, (512,)), (512, 256, (256, 256)), (256, 128, (128, 128)), (256, 128, (128, 128)), (256, 128, (128, 128)), (256, 160, (128, 128))),
     ((256, 0, ()), (512, 0, ()), (512, 0, (1024,)), (256, 0, (512,)), (256, 0, (256,)), (256, 0, (256,))),
 )
-FIRST_GATHERS = (1536, 1536, 640)
+DENSEST = 1536
+FIRST_GATHERS = (2048, 1664)
 HELD_BACK = SLOTS - sum(FIRST_GATHERS)
 LAST_GATHERS = (
     ("scales", 1536),
@@ -58,8 +59,8 @@ def tile_routed_moe_kernel(tc, xT, w_words, w_scales, b, gate, offs, pos1, pos2,
         pos2_sb = lists.tile([P, T // PER_COLUMN], U16, name="pos2_sb")
 
         grouped = [keep.tile([P, T, PACK], BF16, name="grouped%d" % a, align_bytes=ALIGN) for a in range(PASSES)]
-        both_words = keep.tile([P, PASSES * T], U32, name="both_words", align_bytes=ALIGN)
-        words = [both_words[:, T : 2 * T], both_words[:, 0:T]]
+        both_words = keep.tile([P, (PASSES + 1) * T], U32, name="both_words", align_bytes=ALIGN)
+        words = [both_words[:, (1 - a) * T : (2 - a) * T] for a in range(PASSES)]
         scales = keep.tile([P, T], U8, name="scales", align_bytes=ALIGN)
         slot_words = [keep.tile([P, SLOTS - HELD_BACK * (1 - a)], U32, name="slot_words%d" % a, align_bytes=ALIGN) for a in range(PASSES)]
         held_words = []
@@ -118,7 +119,7 @@ def tile_routed_moe_kernel(tc, xT, w_words, w_scales, b, gate, offs, pos1, pos2,
             return slot_words[a][:, cols.start - HELD_BACK : cols.stop - HELD_BACK]
 
         def gather_words(a, s0, n):
-            window = words[a] if n < T else both_words[:]
+            window = words[a] if n <= DENSEST else both_words[:, (1 - a) * T : (3 - a) * T]
             nc.vector.tensor_copy(slots_of(a, slice(s0, s0 + n)), window.indirect(offsets(offs_sb, s0, n)))
 
         def gather_scales(s0, n):

@@ -28,7 +28,7 @@ SILU = mybir.ActivationFunctionType.Silu
 COPY = mybir.ActivationFunctionType.Copy
 
 LOADS = (
-    ((512, 128, (512,)), (512, 256, (256, 256)), (256, 128, (128, 128)), (256, 128, (128, 128)), (256, 128, (128, 128)), (256, 160, (128, 128))),
+    ((512, 0, (512,)), (512, 256, (256, 256)), (256, 128, (128, 128)), (256, 128, (128, 128)), (256, 128, (128, 128)), (256, 160, (128, 128))),
     ((256, 0, ()), (512, 0, ()), (512, 0, (1024,)), (256, 0, (512,)), (256, 0, (256,)), (256, 0, (256,))),
 )
 DENSEST = 1536

@@ -2,6 +2,7 @@ from contextlib import ExitStack
 from itertools import accumulate
 
 import concourse.mybir as mybir
+from concourse.masks import make_identity
 
 K, T, E, C, N = 1024, 2048, 16, 256, 128
 P = 128
@@ -43,8 +44,19 @@ LAST_GATHERS = (
     ("words", 256),
     ("words", 256),
 )
-PIECES = ((640, True), (640, True), (320, False), (256, False), (192, False))
-ON_VECTOR = sum(n for n, on_vector in PIECES if on_vector)
+BANK = 512
+EXPERT_BANKS = 4
+PIECES = (
+    (352, True, True),
+    (512, True, False),
+    (256, False, True),
+    (256, False, True),
+    (480, True, False),
+    (192, True, False),
+)
+LAG = 2
+ON_VECTOR = sum(piece[0] for piece in PIECES if piece[1])
+EARLY_GATES = 4
 
 
 def tile_routed_moe_kernel(tc, xT, w_words, w_scales, b, gate, offs, pos1, pos2, out):
@@ -52,7 +64,7 @@ def tile_routed_moe_kernel(tc, xT, w_words, w_scales, b, gate, offs, pos1, pos2,
     with ExitStack() as ctx:
         lists = ctx.enter_context(tc.tile_pool(name="lists", bufs=1))
         keep = ctx.enter_context(tc.tile_pool(name="keep", bufs=1))
-        psum = ctx.enter_context(tc.psum_pool(name="psum", bufs=4))
+        psum = ctx.enter_context(tc.psum_pool(name="psum", bufs=1))
 
         offs_sb = lists.tile([P, SLOTS // PER_COLUMN], U16, name="offs_sb")
         pos1_sb = lists.tile([P, T // PER_COLUMN], U16, name="pos1_sb")
@@ -70,6 +82,9 @@ def tile_routed_moe_kernel(tc, xT, w_words, w_scales, b, gate, offs, pos1, pos2,
         b_sb = keep.tile([P, E], F32, name="b_sb")
         gate_sb = keep.tile([P, 2, T], F32, name="gate_sb", align_bytes=ALIGN)
         y = keep.tile([P, SLOTS], F32, name="y", align_bytes=ALIGN)
+
+        identity = keep.tile([P, P], F32, name="identity", align_bytes=ALIGN)
+        make_identity(nc, identity[:])
 
         nc.vector.memset(scales[:].bitcast(I32), 0)
         nc.vector.memset(ws_sb[:].rearrange("p e n -> p (e n)").bitcast(I32), 0)
@@ -125,9 +140,12 @@ def tile_routed_moe_kernel(tc, xT, w_words, w_scales, b, gate, offs, pos1, pos2,
         def gather_scales(s0, n):
             nc.vector.tensor_copy(slot_scales[:, s0 : s0 + n], scales[:].indirect(offsets(offs_sb, s0, n)))
 
+        used = []
+
         def expert(e, lo, hi):
             cols = slice(e * C + lo, e * C + hi)
-            acc = psum.tile([P, hi - lo], F32, name="acc")
+            acc = psum.tile([P, hi - lo], F32, name="bank%d" % (len(used) % EXPERT_BANKS))
+            used.append(acc)
             for a in range(PASSES):
                 nc.tensor.matmul_mx(
                     out=acc[:],
@@ -151,19 +169,35 @@ def tile_routed_moe_kernel(tc, xT, w_words, w_scales, b, gate, offs, pos1, pos2,
                     out=ws_sb[row : row + SCALE_ROWS, :, :].bitcast(I32),
                     in_=w_scales[:, a, blocks, :].rearrange("e q n -> q e n").bitcast(I32),
                 )
-        def load_weights(half):
-            experts = slice(half * E // 2, (half + 1) * E // 2)
-            nc.sync.dma_start(
-                out=w_sb[:, experts, :, :].rearrange("p e a n -> p (e a) n"),
-                in_=w_words[experts].rearrange("e a p n r -> p (e a) (n r)").bitcast(I32),
-            )
-
-        load_weights(0)
+        nc.sync.dma_start(gate_sb[:], gate.rearrange("r p t -> p r t"))
+        nc.sync.dma_start(
+            out=w_sb[:].rearrange("p e a n -> p (e a) n"),
+            in_=w_words.rearrange("e a p n r -> p (e a) (n r)").bitcast(I32),
+        )
         nc.sync.dma_start(b_sb[:], b)
         nc.sync.dma_start(pos1_sb[:], pos1)
         nc.sync.dma_start(pos2_sb[:], pos2)
-        nc.sync.dma_start(gate_sb[:], gate.rearrange("r p t -> p r t"))
-        load_weights(1)
+
+        starts = []
+        products = []
+        reached = [ON_VECTOR, 0]
+        for i, (n, on_vector, on_gpsimd) in enumerate(PIECES):
+            r0 = int(on_vector)
+            starts.append(reached[r0])
+            step = min(n, BANK // (2 - r0))
+            products.extend((i, r0, lo, lo + step) for lo in range(0, n, step))
+            reached[r0] += n
+        gates = []
+
+        def move_gate(name):
+            i, r0, lo, hi = products[len(gates)]
+            bank = psum.tile([P, 2 - r0, hi - lo], F32, name=name)
+            for r in range(r0, 2):
+                nc.tensor.matmul(bank[:, r - r0, :], identity[:], gate_sb[:, r, starts[i] + lo : starts[i] + hi], start=True, stop=True)
+            gates.append(bank)
+
+        for j in range(EARLY_GATES):
+            move_gate("gate_bank%d" % j)
 
         for loaded in loads0:
             quantise(0, *loaded)
@@ -190,6 +224,9 @@ def tile_routed_moe_kernel(tc, xT, w_words, w_scales, b, gate, offs, pos1, pos2,
                     expert(e, lo, lo + step)
             started = ready
 
+        for j in range(len(products) - EARLY_GATES):
+            move_gate("bank%d" % ((len(used) - 2 + j) % EXPERT_BANKS))
+
         pos_sb = (pos1_sb, pos2_sb)
 
         def results(r, t0, n):
@@ -198,23 +235,23 @@ def tile_routed_moe_kernel(tc, xT, w_words, w_scales, b, gate, offs, pos1, pos2,
         first = keep.tile([P, ON_VECTOR], F32, name="first", align_bytes=ALIGN)
         nc.vector.tensor_tensor(first[:], results(0, 0, ON_VECTOR), gate_sb[:, 0, 0:ON_VECTOR], MULT)
 
-        def add(t0, n, weighed):
-            summed = keep.tile([P, n], F32, name="total%d" % t0, align_bytes=ALIGN)
-            other = first[:, t0 : t0 + n] if t0 < ON_VECTOR else weighed[:, 1, :]
-            nc.vector.tensor_add(out=summed[:], in0=weighed[:, 0, :], in1=other)
-            nc.sync.dma_start(out=out[:, t0 : t0 + n], in_=summed[:])
+        def add(engine, i):
+            t0, n, weighed = starts[i], PIECES[i][0], plains[i]
+            other = first[:, t0 : t0 + n] if PIECES[i][1] else weighed[:, 1, :]
+            engine.tensor_add(out=weighed[:, 0, :], in0=weighed[:, 0, :], in1=other)
+            nc.sync.dma_start(out=out[:, t0 : t0 + n], in_=weighed[:, 0, :])
 
-        reached = [ON_VECTOR, 0]
-        waiting = None
-        for n, on_vector in PIECES:
-            r0 = int(on_vector)
-            t0 = reached[r0]
-            plain = keep.tile([P, 2 - r0, n], F32, name="plain%d" % t0, align_bytes=ALIGN)
+        plains = [
+            keep.tile([P, 2 - int(on_vector), n], F32, name="plain%d" % i, align_bytes=ALIGN)
+            for i, (n, on_vector, on_gpsimd) in enumerate(PIECES)
+        ]
+        for (i, r0, lo, hi), bank in zip(products, gates):
             for r in range(r0, 2):
-                nc.scalar.activation(out=plain[:, r - r0, :], in_=results(r, t0, n), func=COPY)
-            nc.vector.tensor_tensor(plain[:], plain[:], gate_sb[:, r0:2, t0 : t0 + n], MULT)
-            if waiting:
-                add(*waiting)
-            waiting = (t0, n, plain)
-            reached[r0] += n
-        add(*waiting)
+                nc.scalar.activation(out=plains[i][:, r - r0, lo:hi], in_=results(r, starts[i] + lo, hi - lo), func=COPY)
+            nc.vector.tensor_tensor(plains[i][:, :, lo:hi], plains[i][:, :, lo:hi], bank[:], MULT)
+            if PIECES[i][2]:
+                add(nc.gpsimd, i)
+            if i >= LAG and not PIECES[i - LAG][2]:
+                add(nc.vector, i - LAG)
+        for i in range(len(PIECES) - LAG, len(PIECES)):
+            add(nc.vector, i)

@@ -46,17 +46,8 @@ LAST_GATHERS = (
 )
 BANK = 512
 EXPERT_BANKS = 4
-PIECES = (
-    (352, True, True),
-    (512, True, False),
-    (256, False, True),
-    (256, False, True),
-    (480, True, False),
-    (192, True, False),
-)
-LAG = 2
+PIECES = ((448, True, False), (896, True, True), (256, False, True), (256, False, False), (192, True, False))
 ON_VECTOR = sum(piece[0] for piece in PIECES if piece[1])
-EARLY_GATES = 4
 
 
 def tile_routed_moe_kernel(tc, xT, w_words, w_scales, b, gate, offs, pos1, pos2, out):
@@ -170,10 +161,12 @@ def tile_routed_moe_kernel(tc, xT, w_words, w_scales, b, gate, offs, pos1, pos2,
                     in_=w_scales[:, a, blocks, :].rearrange("e q n -> q e n").bitcast(I32),
                 )
         nc.sync.dma_start(gate_sb[:], gate.rearrange("r p t -> p r t"))
-        nc.sync.dma_start(
-            out=w_sb[:].rearrange("p e a n -> p (e a) n"),
-            in_=w_words.rearrange("e a p n r -> p (e a) (n r)").bitcast(I32),
-        )
+        for half in range(2):
+            experts = slice(half * E // 2, (half + 1) * E // 2)
+            nc.sync.dma_start(
+                out=w_sb[:, experts, :, :].rearrange("p e a n -> p (e a) n"),
+                in_=w_words[experts].rearrange("e a p n r -> p (e a) (n r)").bitcast(I32),
+            )
         nc.sync.dma_start(b_sb[:], b)
         nc.sync.dma_start(pos1_sb[:], pos1)
         nc.sync.dma_start(pos2_sb[:], pos2)
@@ -181,23 +174,21 @@ def tile_routed_moe_kernel(tc, xT, w_words, w_scales, b, gate, offs, pos1, pos2,
         starts = []
         products = []
         reached = [ON_VECTOR, 0]
-        for i, (n, on_vector, on_gpsimd) in enumerate(PIECES):
+        for i, (n, on_vector, from_psum) in enumerate(PIECES):
             r0 = int(on_vector)
             starts.append(reached[r0])
-            step = min(n, BANK // (2 - r0))
-            products.extend((i, r0, lo, lo + step) for lo in range(0, n, step))
+            step = BANK // (2 - r0) if from_psum else n
+            products.extend((i, r0, lo, min(n, lo + step)) for lo in range(0, n, step))
             reached[r0] += n
         gates = []
-
-        def move_gate(name):
-            i, r0, lo, hi = products[len(gates)]
-            bank = psum.tile([P, 2 - r0, hi - lo], F32, name=name)
-            for r in range(r0, 2):
-                nc.tensor.matmul(bank[:, r - r0, :], identity[:], gate_sb[:, r, starts[i] + lo : starts[i] + hi], start=True, stop=True)
-            gates.append(bank)
-
-        for j in range(EARLY_GATES):
-            move_gate("gate_bank%d" % j)
+        for i, r0, lo, hi in products:
+            weights = gate_sb[:, r0:2, starts[i] + lo : starts[i] + hi]
+            if PIECES[i][2]:
+                bank = psum.tile([P, 2 - r0, hi - lo], F32, name="gate_bank%d" % len(gates))
+                for r in range(2 - r0):
+                    nc.tensor.matmul(bank[:, r, :], identity[:], weights[:, r, :], start=True, stop=True)
+                weights = bank[:]
+            gates.append(weights)
 
         for loaded in loads0:
             quantise(0, *loaded)
@@ -224,9 +215,6 @@ def tile_routed_moe_kernel(tc, xT, w_words, w_scales, b, gate, offs, pos1, pos2,
                     expert(e, lo, lo + step)
             started = ready
 
-        for j in range(len(products) - EARLY_GATES):
-            move_gate("bank%d" % ((len(used) - 2 + j) % EXPERT_BANKS))
-
         pos_sb = (pos1_sb, pos2_sb)
 
         def results(r, t0, n):
@@ -243,15 +231,15 @@ def tile_routed_moe_kernel(tc, xT, w_words, w_scales, b, gate, offs, pos1, pos2,
 
         plains = [
             keep.tile([P, 2 - int(on_vector), n], F32, name="plain%d" % i, align_bytes=ALIGN)
-            for i, (n, on_vector, on_gpsimd) in enumerate(PIECES)
+            for i, (n, on_vector, from_psum) in enumerate(PIECES)
         ]
-        for (i, r0, lo, hi), bank in zip(products, gates):
+        for (i, r0, lo, hi), weights in zip(products, gates):
             for r in range(r0, 2):
                 nc.scalar.activation(out=plains[i][:, r - r0, lo:hi], in_=results(r, starts[i] + lo, hi - lo), func=COPY)
-            nc.vector.tensor_tensor(plains[i][:, :, lo:hi], plains[i][:, :, lo:hi], bank[:], MULT)
-            if PIECES[i][2]:
-                add(nc.gpsimd, i)
-            if i >= LAG and not PIECES[i - LAG][2]:
-                add(nc.vector, i - LAG)
-        for i in range(len(PIECES) - LAG, len(PIECES)):
-            add(nc.vector, i)
+            nc.vector.tensor_tensor(plains[i][:, :, lo:hi], plains[i][:, :, lo:hi], weights, MULT)
+            if hi == PIECES[i][0]:
+                if i == 0:
+                    add(nc.gpsimd, i)
+                if i >= 2:
+                    add(nc.vector, i - 1)
+        add(nc.vector, len(PIECES) - 1)

@@ -29,7 +29,7 @@ SILU = mybir.ActivationFunctionType.Silu
 COPY = mybir.ActivationFunctionType.Copy
 
 LOADS = (
-    ((512, 0, (512,)), (512, 256, (256, 256)), (256, 128, (128, 128)), (256, 128, (128, 128)), (256, 128, (128, 128)), (256, 160, (128, 128))),
+    ((768, 448, (256, 512)), (512, 256, (256, 256)), (256, 128, (128, 128)), (256, 128, (128, 128)), (256, 160, (128, 128))),
     ((256, 0, ()), (512, 0, ()), (512, 0, (1024,)), (256, 0, (512,)), (256, 0, (256,)), (256, 0, (256,))),
 )
 DENSEST = 1536
@@ -160,7 +160,8 @@ def tile_routed_moe_kernel(tc, xT, w_words, w_scales, b, gate, offs, pos1, pos2,
                     out=ws_sb[row : row + SCALE_ROWS, :, :].bitcast(I32),
                     in_=w_scales[:, a, blocks, :].rearrange("e q n -> q e n").bitcast(I32),
                 )
-        nc.sync.dma_start(gate_sb[:], gate.rearrange("r p t -> p r t"))
+        for r in range(2):
+            nc.sync.dma_start(gate_sb[:, r, :], gate[r])
         for half in range(2):
             experts = slice(half * E // 2, (half + 1) * E // 2)
             nc.sync.dma_start(

@@ -241,6 +241,7 @@ def tile_routed_moe_kernel(tc, xT, w_words, w_scales, b, gate, offs, pos1, pos2,
             if hi == PIECES[i][0]:
                 if i == 0:
                     add(nc.gpsimd, i)
-                if i >= 2:
-                    add(nc.vector, i - 1)
-        add(nc.vector, len(PIECES) - 1)
+                if i == 2:
+                    add(nc.vector, 1)
+        for i in range(2, len(PIECES)):
+            add(nc.vector, i)

@@ -30,7 +30,7 @@ COPY = mybir.ActivationFunctionType.Copy
 
 LOADS = (
     ((768, 448, (256, 512)), (512, 256, (256, 256)), (256, 128, (128, 128)), (256, 128, (128, 128)), (256, 160, (128, 128))),
-    ((256, 0, ()), (512, 0, ()), (512, 0, (1024,)), (256, 0, (512,)), (256, 0, (256,)), (256, 0, (256,))),
+    ((512, 0, ()), (512, 0, (1024,)), (512, 0, (512,)), (512, 0, (256, 256))),
 )
 DENSEST = 1536
 FIRST_GATHERS = (2048, 1664)
@@ -69,7 +69,7 @@ def tile_routed_moe_kernel(tc, xT, w_words, w_scales, b, gate, offs, pos1, pos2,
         held_words = []
         slot_scales = keep.tile([P, SLOTS], U8, name="slot_scales", align_bytes=ALIGN)
         w_sb = keep.tile([P, E, PASSES, N], I32, name="w_sb", align_bytes=ALIGN)
-        ws_sb = keep.tile([P, E, N], U8, name="ws_sb", align_bytes=ALIGN)
+        ws_sb = keep.tile([P, E, PASSES, N], U8, name="ws_sb", align_bytes=ALIGN)
         b_sb = keep.tile([P, E], F32, name="b_sb")
         gate_sb = keep.tile([P, 2, T], F32, name="gate_sb", align_bytes=ALIGN)
         y = keep.tile([P, SLOTS], F32, name="y", align_bytes=ALIGN)
@@ -78,7 +78,7 @@ def tile_routed_moe_kernel(tc, xT, w_words, w_scales, b, gate, offs, pos1, pos2,
         make_identity(nc, identity[:])
 
         nc.vector.memset(scales[:].bitcast(I32), 0)
-        nc.vector.memset(ws_sb[:].rearrange("p e n -> p (e n)").bitcast(I32), 0)
+        nc.vector.memset(ws_sb[:].rearrange("p e a n -> p (e a n)").bitcast(I32), 0)
 
         def offsets(list_sb, first, n):
             return list_sb[:, first // PER_COLUMN : (first + n) // PER_COLUMN]
@@ -141,7 +141,7 @@ def tile_routed_moe_kernel(tc, xT, w_words, w_scales, b, gate, offs, pos1, pos2,
                 nc.tensor.matmul_mx(
                     out=acc[:],
                     lhsT=w_sb[:, e, a, :].bitcast(FP8X4),
-                    lhsT_scale=ws_sb[SCALE_ROW[a] : P, e, :],
+                    lhsT_scale=ws_sb[:, e, a, :],
                     rhs=slots_of(a, cols).bitcast(FP8X4),
                     rhs_scale=slot_scales[SCALE_ROW[a] : P, cols],
                     start=(a == 0),
@@ -152,22 +152,18 @@ def tile_routed_moe_kernel(tc, xT, w_words, w_scales, b, gate, offs, pos1, pos2,
         loads0 = load(0)
         nc.sync.dma_start(offs_sb[:], offs)
         loads1 = load(1)
-        for a in range(PASSES):
-            for q in range(P // QUADRANT):
-                row = QUADRANT * q + SCALE_ROW[a]
-                blocks = slice(SCALE_ROWS * q, SCALE_ROWS * (q + 1))
-                nc.sync.dma_start(
-                    out=ws_sb[row : row + SCALE_ROWS, :, :].bitcast(I32),
-                    in_=w_scales[:, a, blocks, :].rearrange("e q n -> q e n").bitcast(I32),
-                )
-        for r in range(2):
-            nc.sync.dma_start(gate_sb[:, r, :], gate[r])
-        for half in range(2):
-            experts = slice(half * E // 2, (half + 1) * E // 2)
+        for q in range(P // QUADRANT):
+            row = QUADRANT * q
+            blocks = slice(SCALE_ROWS * q, SCALE_ROWS * (q + 1))
             nc.sync.dma_start(
-                out=w_sb[:, experts, :, :].rearrange("p e a n -> p (e a) n"),
-                in_=w_words[experts].rearrange("e a p n r -> p (e a) (n r)").bitcast(I32),
+                out=ws_sb[row : row + SCALE_ROWS, :, :, :].rearrange("q e a n -> q (e a) n").bitcast(I32),
+                in_=w_scales[:, :, blocks, :].rearrange("e a q n -> q (e a) n").bitcast(I32),
             )
+        nc.sync.dma_start(gate_sb[:], gate.rearrange("r p t -> p r t"))
+        nc.sync.dma_start(
+            out=w_sb[:].rearrange("p e a n -> p (e a) n"),
+            in_=w_words.rearrange("e a p n r -> p (e a) (n r)").bitcast(I32),
+        )
         nc.sync.dma_start(b_sb[:], b)
         nc.sync.dma_start(pos1_sb[:], pos1)
         nc.sync.dma_start(pos2_sb[:], pos2)

@@ -46,8 +46,8 @@ LAST_GATHERS = (
 )
 BANK = 512
 EXPERT_BANKS = 4
-PIECES = ((448, True, False), (896, True, True), (256, False, True), (256, False, False), (192, True, False))
-ON_VECTOR = sum(piece[0] for piece in PIECES if piece[1])
+ON_VECTOR = 736
+PIECES = ((512, True), (384, True), (256, False), (160, False))
 
 
 def tile_routed_moe_kernel(tc, xT, w_words, w_scales, b, gate, offs, pos1, pos2, out):
@@ -168,24 +168,18 @@ def tile_routed_moe_kernel(tc, xT, w_words, w_scales, b, gate, offs, pos1, pos2,
         nc.sync.dma_start(pos1_sb[:], pos1)
         nc.sync.dma_start(pos2_sb[:], pos2)
 
-        starts = []
+        starts = list(accumulate((piece[0] for piece in PIECES), initial=ON_VECTOR))
         products = []
-        reached = [ON_VECTOR, 0]
-        for i, (n, on_vector, from_psum) in enumerate(PIECES):
-            r0 = int(on_vector)
-            starts.append(reached[r0])
-            step = BANK // (2 - r0) if from_psum else n
-            products.extend((i, r0, lo, min(n, lo + step)) for lo in range(0, n, step))
-            reached[r0] += n
-        gates = []
-        for i, r0, lo, hi in products:
-            weights = gate_sb[:, r0:2, starts[i] + lo : starts[i] + hi]
-            if PIECES[i][2]:
-                bank = psum.tile([P, 2 - r0, hi - lo], F32, name="gate_bank%d" % len(gates))
-                for r in range(2 - r0):
-                    nc.tensor.matmul(bank[:, r, :], identity[:], weights[:, r, :], start=True, stop=True)
-                weights = bank[:]
-            gates.append(weights)
+        for i, (n, from_psum) in enumerate(PIECES):
+            step = 1 if 2 * n > BANK else 2
+            for r0 in range(0, 2, step):
+                weights = gate_sb[:, r0 : r0 + step, starts[i] : starts[i] + n]
+                if from_psum:
+                    bank = psum.tile([P, step, n], F32, name="gate_bank%d" % len(products))
+                    for r in range(step):
+                        nc.tensor.matmul(bank[:, r, :], identity[:], weights[:, r, :], start=True, stop=True)
+                    weights = bank[:]
+                products.append((i, range(r0, r0 + step), weights))
 
         for loaded in loads0:
             quantise(0, *loaded)
@@ -217,27 +211,22 @@ def tile_routed_moe_kernel(tc, xT, w_words, w_scales, b, gate, offs, pos1, pos2,
         def results(r, t0, n):
             return y[:].indirect(offsets(pos_sb[r], t0, n))
 
-        first = keep.tile([P, ON_VECTOR], F32, name="first", align_bytes=ALIGN)
-        nc.vector.tensor_tensor(first[:], results(0, 0, ON_VECTOR), gate_sb[:, 0, 0:ON_VECTOR], MULT)
+        def add(engine, pairs, t0):
+            engine.tensor_add(out=pairs[:, 0, :], in0=pairs[:, 0, :], in1=pairs[:, 1, :])
+            nc.sync.dma_start(out=out[:, t0 : t0 + pairs.shape[2]], in_=pairs[:, 0, :])
 
-        def add(engine, i):
-            t0, n, weighed = starts[i], PIECES[i][0], plains[i]
-            other = first[:, t0 : t0 + n] if PIECES[i][1] else weighed[:, 1, :]
-            engine.tensor_add(out=weighed[:, 0, :], in0=weighed[:, 0, :], in1=other)
-            nc.sync.dma_start(out=out[:, t0 : t0 + n], in_=weighed[:, 0, :])
+        fused = keep.tile([P, 2, ON_VECTOR], F32, name="fused", align_bytes=ALIGN)
+        for r in range(2):
+            nc.vector.tensor_tensor(fused[:, r, :], results(r, 0, ON_VECTOR), gate_sb[:, r, 0:ON_VECTOR], MULT)
+        add(nc.gpsimd, fused[:], 0)
 
-        plains = [
-            keep.tile([P, 2 - int(on_vector), n], F32, name="plain%d" % i, align_bytes=ALIGN)
-            for i, (n, on_vector, from_psum) in enumerate(PIECES)
-        ]
-        for (i, r0, lo, hi), weights in zip(products, gates):
-            for r in range(r0, 2):
-                nc.scalar.activation(out=plains[i][:, r - r0, lo:hi], in_=results(r, starts[i] + lo, hi - lo), func=COPY)
-            nc.vector.tensor_tensor(plains[i][:, :, lo:hi], plains[i][:, :, lo:hi], weights, MULT)
-            if hi == PIECES[i][0]:
-                if i == 0:
-                    add(nc.gpsimd, i)
-                if i == 2:
-                    add(nc.vector, 1)
-        for i in range(2, len(PIECES)):
-            add(nc.vector, i)
+        plains = [keep.tile([P, 2, n], F32, name="plain%d" % i, align_bytes=ALIGN) for i, (n, from_psum) in enumerate(PIECES)]
+        plains = [tile[:] for tile in plains]
+        for i, rs, weights in products:
+            for r in rs:
+                nc.scalar.activation(out=plains[i][:, r, :], in_=results(r, starts[i], PIECES[i][0]), func=COPY)
+            pair = plains[i][:, rs.start : rs.stop, :]
+            nc.vector.tensor_tensor(pair, pair, weights, MULT)
+            if i > 0 and rs.stop == 2:
+                add(nc.vector, plains[i - 1], starts[i - 1])
+        add(nc.vector, plains[-1], starts[-2])

@@ -30,7 +30,7 @@ COPY = mybir.ActivationFunctionType.Copy
 
 LOADS = (
     ((768, 448, (256, 512)), (512, 256, (256, 256)), (256, 128, (128, 128)), (256, 128, (128, 128)), (256, 160, (128, 128))),
-    ((512, 0, ()), (512, 0, (1024,)), (512, 0, (512,)), (512, 0, (256, 256))),
+    tuple((256, 0, widths) for widths in ((), (), (), (1024,), (), (512,), (256,), (256,))),
 )
 DENSEST = 1536
 FIRST_GATHERS = (2048, 1664)
@@ -69,7 +69,7 @@ def tile_routed_moe_kernel(tc, xT, w_words, w_scales, b, gate, offs, pos1, pos2,
         held_words = []
         slot_scales = keep.tile([P, SLOTS], U8, name="slot_scales", align_bytes=ALIGN)
         w_sb = keep.tile([P, E, PASSES, N], I32, name="w_sb", align_bytes=ALIGN)
-        ws_sb = keep.tile([P, E, PASSES, N], U8, name="ws_sb", align_bytes=ALIGN)
+        ws_sb = keep.tile([P, E, N], U8, name="ws_sb", align_bytes=ALIGN)
         b_sb = keep.tile([P, E], F32, name="b_sb")
         gate_sb = keep.tile([P, 2, T], F32, name="gate_sb", align_bytes=ALIGN)
         y = keep.tile([P, SLOTS], F32, name="y", align_bytes=ALIGN)
@@ -78,7 +78,7 @@ def tile_routed_moe_kernel(tc, xT, w_words, w_scales, b, gate, offs, pos1, pos2,
         make_identity(nc, identity[:])
 
         nc.vector.memset(scales[:].bitcast(I32), 0)
-        nc.vector.memset(ws_sb[:].rearrange("p e a n -> p (e a n)").bitcast(I32), 0)
+        nc.vector.memset(ws_sb[:].rearrange("p e n -> p (e n)").bitcast(I32), 0)
 
         def offsets(list_sb, first, n):
             return list_sb[:, first // PER_COLUMN : (first + n) // PER_COLUMN]
@@ -141,7 +141,7 @@ def tile_routed_moe_kernel(tc, xT, w_words, w_scales, b, gate, offs, pos1, pos2,
                 nc.tensor.matmul_mx(
                     out=acc[:],
                     lhsT=w_sb[:, e, a, :].bitcast(FP8X4),
-                    lhsT_scale=ws_sb[:, e, a, :],
+                    lhsT_scale=ws_sb[SCALE_ROW[a] : P, e, :],
                     rhs=slots_of(a, cols).bitcast(FP8X4),
                     rhs_scale=slot_scales[SCALE_ROW[a] : P, cols],
                     start=(a == 0),
@@ -152,13 +152,14 @@ def tile_routed_moe_kernel(tc, xT, w_words, w_scales, b, gate, offs, pos1, pos2,
         loads0 = load(0)
         nc.sync.dma_start(offs_sb[:], offs)
         loads1 = load(1)
-        for q in range(P // QUADRANT):
-            row = QUADRANT * q
-            blocks = slice(SCALE_ROWS * q, SCALE_ROWS * (q + 1))
-            nc.sync.dma_start(
-                out=ws_sb[row : row + SCALE_ROWS, :, :, :].rearrange("q e a n -> q (e a) n").bitcast(I32),
-                in_=w_scales[:, :, blocks, :].rearrange("e a q n -> q (e a) n").bitcast(I32),
-            )
+        for a in range(PASSES):
+            for q in range(P // QUADRANT):
+                row = QUADRANT * q + SCALE_ROW[a]
+                blocks = slice(SCALE_ROWS * q, SCALE_ROWS * (q + 1))
+                nc.sync.dma_start(
+                    out=ws_sb[row : row + SCALE_ROWS, :, :].bitcast(I32),
+                    in_=w_scales[:, a, blocks, :].rearrange("e q n -> q e n").bitcast(I32),
+                )
         nc.sync.dma_start(gate_sb[:], gate.rearrange("r p t -> p r t"))
         nc.sync.dma_start(
             out=w_sb[:].rearrange("p e a n -> p (e a) n"),

@@ -33,7 +33,7 @@ LOADS = (
     tuple((256, 0, widths) for widths in ((), (), (), (1024,), (), (512,), (256,), (256,))),
 )
 DENSEST = 1536
-FIRST_GATHERS = (2048, 1664)
+FIRST_GATHERS = (2048, 1536)
 HELD_BACK = SLOTS - sum(FIRST_GATHERS)
 LAST_GATHERS = (
     ("scales", 1536),
@@ -202,7 +202,7 @@ def tile_routed_moe_kernel(tc, xT, w_words, w_scales, b, gate, offs, pos1, pos2,
             gathered[what] += n
             ready = min(gathered.values()) // C
             for e in range(started, ready):
-                step = C // 2 if e in (HELD_BACK // C, E - 1) else C
+                step = C // 2 if e == E - 1 else C
                 for lo in range(0, C, step):
                     expert(e, lo, lo + step)
             started = ready

@@ -47,7 +47,7 @@ LAST_GATHERS = (
 BANK = 512
 EXPERT_BANKS = 4
 ON_VECTOR = 736
-PIECES = ((512, True), (384, True), (256, False), (160, False))
+PIECES = ((512, True), (448, True), (192, False), (160, False))
 
 
 def tile_routed_moe_kernel(tc, xT, w_words, w_scales, b, gate, offs, pos1, pos2, out):
@@ -221,13 +221,14 @@ def tile_routed_moe_kernel(tc, xT, w_words, w_scales, b, gate, offs, pos1, pos2,
             nc.vector.tensor_tensor(fused[:, r, :], results(r, 0, ON_VECTOR), gate_sb[:, r, 0:ON_VECTOR], MULT)
         add(nc.gpsimd, fused[:], 0)
 
-        plains = [keep.tile([P, 2, n], F32, name="plain%d" % i, align_bytes=ALIGN) for i, (n, from_psum) in enumerate(PIECES)]
-        plains = [tile[:] for tile in plains]
+        plains = [
+            keep.tile([P, 2, n], F32, name="plain%d" % i, align_bytes=ALIGN) for i, (n, from_psum) in enumerate(PIECES)
+        ]
         for i, rs, weights in products:
             for r in rs:
                 nc.scalar.activation(out=plains[i][:, r, :], in_=results(r, starts[i], PIECES[i][0]), func=COPY)
             pair = plains[i][:, rs.start : rs.stop, :]
             nc.vector.tensor_tensor(pair, pair, weights, MULT)
-            if i > 0 and rs.stop == 2:
-                add(nc.vector, plains[i - 1], starts[i - 1])
-        add(nc.vector, plains[-1], starts[-2])
+            if i % 2 == 1 and rs.stop == 2:
+                for done in (i - 1, i):
+                    add(nc.vector, plains[done][:], starts[done])

from contextlib import ExitStack
from itertools import accumulate

import concourse.mybir as mybir
from concourse.masks import make_identity

K, T, E, C, N = 1024, 2048, 16, 256, 128
P = 128
PACK = 4
K_PASS = P * PACK
PASSES = K // K_PASS
SLOTS = E * C
PER_COLUMN = 16
QUADRANT = 32
SCALE_ROWS = 4
SCALE_ROW = (SCALE_ROWS, 0)
ALIGN = 256
FLOPS = 2 * SLOTS * K * N

F32 = mybir.dt.float32
BF16 = mybir.dt.bfloat16
I32 = mybir.dt.int32
U32 = mybir.dt.uint32
U16 = mybir.dt.uint16
U8 = mybir.dt.uint8
FP8X4 = mybir.dt.float8_e4m3fn_x4
MULT = mybir.AluOpType.mult
SILU = mybir.ActivationFunctionType.Silu
COPY = mybir.ActivationFunctionType.Copy

LOADS = (
    ((768, 448, (256, 512)), (512, 256, (256, 256)), (256, 128, (128, 128)), (256, 128, (128, 128)), (256, 160, (128, 128))),
    tuple((256, 0, widths) for widths in ((), (), (), (1024,), (), (512,), (256,), (256,))),
)
DENSEST = 1536
FIRST_GATHERS = (2048, 1536)
HELD_BACK = SLOTS - sum(FIRST_GATHERS)
LAST_GATHERS = (
    ("scales", 1536),
    ("scales", 1536),
    ("words", 2048),
    ("words", 1536),
    ("scales", 1024),
    ("words", 256),
    ("words", 256),
)
BANK = 512
EXPERT_BANKS = 4
ON_VECTOR = 736
PIECES = ((512, True), (448, True), (192, False), (160, False))


def tile_routed_moe_kernel(tc, xT, w_words, w_scales, b, gate, offs, pos1, pos2, out):
    nc = tc.nc
    with ExitStack() as ctx:
        lists = ctx.enter_context(tc.tile_pool(name="lists", bufs=1))
        keep = ctx.enter_context(tc.tile_pool(name="keep", bufs=1))
        psum = ctx.enter_context(tc.psum_pool(name="psum", bufs=1))

        offs_sb = lists.tile([P, SLOTS // PER_COLUMN], U16, name="offs_sb")
        pos1_sb = lists.tile([P, T // PER_COLUMN], U16, name="pos1_sb")
        pos2_sb = lists.tile([P, T // PER_COLUMN], U16, name="pos2_sb")

        grouped = [keep.tile([P, T, PACK], BF16, name="grouped%d" % a, align_bytes=ALIGN) for a in range(PASSES)]
        both_words = keep.tile([P, (PASSES + 1) * T], U32, name="both_words", align_bytes=ALIGN)
        words = [both_words[:, (1 - a) * T : (2 - a) * T] for a in range(PASSES)]
        scales = keep.tile([P, T], U8, name="scales", align_bytes=ALIGN)
        slot_words = [keep.tile([P, SLOTS - HELD_BACK * (1 - a)], U32, name="slot_words%d" % a, align_bytes=ALIGN) for a in range(PASSES)]
        held_words = []
        slot_scales = keep.tile([P, SLOTS], U8, name="slot_scales", align_bytes=ALIGN)
        w_sb = keep.tile([P, E, PASSES, N], I32, name="w_sb", align_bytes=ALIGN)
        ws_sb = keep.tile([P, E, N], U8, name="ws_sb", align_bytes=ALIGN)
        b_sb = keep.tile([P, E], F32, name="b_sb")
        gate_sb = keep.tile([P, 2, T], F32, name="gate_sb", align_bytes=ALIGN)
        y = keep.tile([P, SLOTS], F32, name="y", align_bytes=ALIGN)

        identity = keep.tile([P, P], F32, name="identity", align_bytes=ALIGN)
        make_identity(nc, identity[:])

        nc.vector.memset(scales[:].bitcast(I32), 0)
        nc.vector.memset(ws_sb[:].rearrange("p e n -> p (e n)").bitcast(I32), 0)

        def offsets(list_sb, first, n):
            return list_sb[:, first // PER_COLUMN : (first + n) // PER_COLUMN]

        def load(a):
            loaded = []
            t0 = 0
            rows = xT[a * K_PASS : (a + 1) * K_PASS, :].rearrange("(p j) t -> p j t", j=PACK)
            for n, on_vector, widths in LOADS[a]:
                raw = keep.tile([P, PACK, n], F32, name="raw%d_%d" % (a, t0), align_bytes=ALIGN)
                nc.sync.dma_start(out=raw[:], in_=rows[:, :, t0 : t0 + n])
                loaded.append((raw, t0, n, on_vector, widths))
                t0 += n
            return loaded

        def interleave(copy, a, raw, t0, lo, hi):
            copy(
                out=grouped[a][:, t0 + lo : t0 + hi, :].rearrange("p (c i) j -> p c j i", i=4),
                in_=raw[:, :, lo:hi].rearrange("p j (c i) -> p c j i", i=4),
            )

        quantised = [0] * PASSES

        def quantise(a, raw, t0, n, on_vector, widths):
            cuts = [c - t0 for c in accumulate(widths, initial=quantised[a]) if t0 + on_vector < c < t0 + n]
            for lo, hi in zip([on_vector] + cuts, cuts + [n]):
                interleave(nc.scalar.copy, a, raw, t0, lo, hi)
            if on_vector:
                interleave(nc.vector.tensor_copy, a, raw, t0, 0, on_vector)
            for m in widths:
                lo = quantised[a]
                nc.vector.quantize_mx(
                    out=words[a][:, lo : lo + m].bitcast(FP8X4),
                    scales=scales[SCALE_ROW[a] : P, lo : lo + m],
                    in_=grouped[a][:, lo : lo + m, :].rearrange("p t j -> p (t j)"),
                )
                quantised[a] = lo + m

        def slots_of(a, cols):
            if a == 1:
                return slot_words[a][:, cols]
            if cols.start < HELD_BACK:
                return held_words[0][:, cols]
            return slot_words[a][:, cols.start - HELD_BACK : cols.stop - HELD_BACK]

        def gather_words(a, s0, n):
            window = words[a] if n <= DENSEST else both_words[:, (1 - a) * T : (3 - a) * T]
            nc.vector.tensor_copy(slots_of(a, slice(s0, s0 + n)), window.indirect(offsets(offs_sb, s0, n)))

        def gather_scales(s0, n):
            nc.vector.tensor_copy(slot_scales[:, s0 : s0 + n], scales[:].indirect(offsets(offs_sb, s0, n)))

        used = []

        def expert(e, lo, hi):
            cols = slice(e * C + lo, e * C + hi)
            acc = psum.tile([P, hi - lo], F32, name="bank%d" % (len(used) % EXPERT_BANKS))
            used.append(acc)
            for a in range(PASSES):
                nc.tensor.matmul_mx(
                    out=acc[:],
                    lhsT=w_sb[:, e, a, :].bitcast(FP8X4),
                    lhsT_scale=ws_sb[SCALE_ROW[a] : P, e, :],
                    rhs=slots_of(a, cols).bitcast(FP8X4),
                    rhs_scale=slot_scales[SCALE_ROW[a] : P, cols],
                    start=(a == 0),
                    stop=(a == PASSES - 1),
                )
            nc.scalar.activation(out=y[:, cols], in_=acc[:], func=SILU, bias=b_sb[:, e : e + 1])

        loads0 = load(0)
        nc.sync.dma_start(offs_sb[:], offs)
        loads1 = load(1)
        for a in range(PASSES):
            for q in range(P // QUADRANT):
                row = QUADRANT * q + SCALE_ROW[a]
                blocks = slice(SCALE_ROWS * q, SCALE_ROWS * (q + 1))
                nc.sync.dma_start(
                    out=ws_sb[row : row + SCALE_ROWS, :, :].bitcast(I32),
                    in_=w_scales[:, a, blocks, :].rearrange("e q n -> q e n").bitcast(I32),
                )
        nc.sync.dma_start(gate_sb[:], gate.rearrange("r p t -> p r t"))
        nc.sync.dma_start(
            out=w_sb[:].rearrange("p e a n -> p (e a) n"),
            in_=w_words.rearrange("e a p n r -> p (e a) (n r)").bitcast(I32),
        )
        nc.sync.dma_start(b_sb[:], b)
        nc.sync.dma_start(pos1_sb[:], pos1)
        nc.sync.dma_start(pos2_sb[:], pos2)

        starts = list(accumulate((piece[0] for piece in PIECES), initial=ON_VECTOR))
        products = []
        for i, (n, from_psum) in enumerate(PIECES):
            step = 1 if 2 * n > BANK else 2
            for r0 in range(0, 2, step):
                weights = gate_sb[:, r0 : r0 + step, starts[i] : starts[i] + n]
                if from_psum:
                    bank = psum.tile([P, step, n], F32, name="gate_bank%d" % len(products))
                    for r in range(step):
                        nc.tensor.matmul(bank[:, r, :], identity[:], weights[:, r, :], start=True, stop=True)
                    weights = bank[:]
                products.append((i, range(r0, r0 + step), weights))

        for loaded in loads0:
            quantise(0, *loaded)
        s0 = HELD_BACK
        for n in FIRST_GATHERS:
            gather_words(0, s0, n)
            s0 += n
        for loaded in loads1:
            quantise(1, *loaded)
        held_words.append(keep.tile([P, HELD_BACK], U32, name="raw1_%d" % loads1[-1][1], align_bytes=ALIGN))
        gather_words(0, 0, HELD_BACK)
        gathered = {"scales": 0, "words": 0}
        started = 0
        for what, n in LAST_GATHERS:
            if what == "scales":
                gather_scales(gathered[what], n)
            else:
                gather_words(1, gathered[what], n)
            gathered[what] += n
            ready = min(gathered.values()) // C
            for e in range(started, ready):
                step = C // 2 if e == E - 1 else C
                for lo in range(0, C, step):
                    expert(e, lo, lo + step)
            started = ready

        pos_sb = (pos1_sb, pos2_sb)

        def results(r, t0, n):
            return y[:].indirect(offsets(pos_sb[r], t0, n))

        def add(engine, pairs, t0):
            engine.tensor_add(out=pairs[:, 0, :], in0=pairs[:, 0, :], in1=pairs[:, 1, :])
            nc.sync.dma_start(out=out[:, t0 : t0 + pairs.shape[2]], in_=pairs[:, 0, :])

        fused = keep.tile([P, 2, ON_VECTOR], F32, name="fused", align_bytes=ALIGN)
        for r in range(2):
            nc.vector.tensor_tensor(fused[:, r, :], results(r, 0, ON_VECTOR), gate_sb[:, r, 0:ON_VECTOR], MULT)
        add(nc.gpsimd, fused[:], 0)

        plains = [
            keep.tile([P, 2, n], F32, name="plain%d" % i, align_bytes=ALIGN) for i, (n, from_psum) in enumerate(PIECES)
        ]
        for i, rs, weights in products:
            for r in rs:
                nc.scalar.activation(out=plains[i][:, r, :], in_=results(r, starts[i], PIECES[i][0]), func=COPY)
            pair = plains[i][:, rs.start : rs.stop, :]
            nc.vector.tensor_tensor(pair, pair, weights, MULT)
            if i % 2 == 1 and rs.stop == 2:
                for done in (i - 1, i):
                    add(nc.vector, plains[done][:], starts[done])
